import numpy as np
import ml_dtypes


def mxq(x, axis, fmt="e4m3"):
    dtype, down = {"e4m3": (ml_dtypes.float8_e4m3fn, 7), "e5m2": (ml_dtypes.float8_e5m2, 14)}[fmt]
    v = np.moveaxis(np.asarray(x, np.float32).astype(ml_dtypes.bfloat16).astype(np.float64), axis, -1)
    blocks = v.reshape(v.shape[:-1] + (-1, 32))
    amax = np.abs(blocks).max(-1, keepdims=True)
    byte = np.maximum(np.where(amax > 0, np.frexp(amax)[1] - 1 + 127, 0) - down, 1)
    scale = np.exp2(byte - 127.0)
    codes = (blocks / scale).astype(np.float32).astype(dtype).astype(np.float64)
    return np.moveaxis((codes * scale).reshape(v.shape), -1, axis)


WIDE = False


def mx_kscale(k):
    if not WIDE:
        return np.ones(k)
    levels = np.array([10, -10, 5, -5, 0])
    if k % 512:
        return np.exp2(np.random.permutation(np.resize(levels, k // 32))).repeat(32)
    a = np.empty((k // 512, 16))
    for p in range(k // 512):
        a[p, :8] = np.random.permutation(np.resize(levels, 8))
        for g in range(8):
            far = levels[np.abs(levels - a[p, g]) >= 10]
            a[p, g + 8] = far[np.random.randint(len(far))]
    return np.exp2(a.ravel()).repeat(32)


BF16 = ml_dtypes.bfloat16


def bf(x):
    return np.asarray(x, np.float32).astype(BF16)


def f64(x):
    return np.asarray(x).astype(np.float64)

def planes(Y):
    n, m = Y.shape
    b = f64(bf(Y)).reshape(n // 32, 32, m)
    amax = np.abs(b).max(1)
    byte = np.clip(np.where(amax > 0, np.frexp(amax)[1] - 1 + 127 - 7, 1), 1, 254)
    codes = (b * np.exp2(127.0 - byte)[:, None, :]).reshape(n, m).astype(np.float32).astype(ml_dtypes.float8_e4m3fn).view(np.uint8)
    words = codes.reshape(n // 512, 128, 4, m).transpose(0, 1, 3, 2)
    return np.ascontiguousarray(words), np.ascontiguousarray(byte.astype(np.uint8).reshape(n // 512, 16, m))


N, C, W, QN = 1024, 1024, 1024, 1024


def co_degree(co, idfc):
    return idfc[:, None] * np.log(1.0 + np.maximum(co, 0.0))


def setup_inputs():
    s, t = mx_kscale(N), mx_kscale(W)
    return {
        "tfc": bf(np.random.standard_normal((N, C)) * 1.5 * s[:, None]),
        "tfw": bf(np.random.standard_normal((N, W)) * 1.5 / s[:, None]),
        "idfc": bf(np.random.uniform(0.5, 2.5, C)),
        "idfw": bf(np.random.uniform(0.5, 1.5, W) * t),
        "q": bf(np.random.standard_normal((QN, W)) / np.sqrt(W) / t),
    }


def core(tfc, tfw, idfc, idfw, q):
    n = tfc.shape[0]
    co = (mxq(f64(tfc), 0, "e4m3").T @ mxq(f64(tfw), 0, "e4m3")) / np.sqrt(n)
    deg = co_degree(co, f64(idfc))
    f = np.log(0.1 + deg)
    h = f * f64(idfw)[None, :]
    return mxq(f64(q), 1, "e4m3") @ mxq(h, 1, "e4m3").T


def reference(tfc, tfw, idfc, idfw, q):
    R_out = core(tfc, tfw, idfc, idfw, q)
    words, scales = planes(R_out.T)
    return R_out, words, scales

@@ -1,0 +1,381 @@
+from contextlib import ExitStack
+
+import concourse.mybir as mybir
+from concourse.masks import make_identity
+
+F32 = mybir.dt.float32
+BF16 = mybir.dt.bfloat16
+U32 = mybir.dt.uint32
+I32 = mybir.dt.int32
+U8 = mybir.dt.uint8
+FP8X4 = mybir.dt.float8_e4m3fn_x4
+ACT = mybir.ActivationFunctionType
+ALU = mybir.AluOpType
+
+SIZE = 1024
+P = 128
+PACK = 4
+K_PASS = P * PACK
+PASSES = SIZE // K_PASS
+BANK = 512
+CHUNK = 256
+STRIPS = SIZE // CHUNK
+FLOPS = 2 * 2 * SIZE * SIZE * SIZE
+
+UNITS = [(0, 0), (1, 0), (2, 0), (3, 0), (0, 1), (1, 1), (2, 1), (3, 1),
+         (4, 0), (5, 0), (4, 1), (5, 1), (6, 0), (7, 0), (6, 1), (7, 1)]
+MANUAL = False
+POOL_BUFS = 2
+R_BUFS = 6
+PAR = {
+    "loads": [["w",0,0,1],["c",0,0,1],["w",1,0,1],["c",1,0,1],["c",0,1,1],["c",1,1,1],["w",0,1,1],["w",1,1,1],["q",0,0,1],["q",0,1,1],["q",0,2,1],["q",0,3,1],["c",0,2,2],["c",1,2,2]],
+    "chunks": [["w",0,0],["w",0,1],["c",0,0],["w",1,0],["w",1,1],["c",1,0],["c",0,1],["c",1,1],["w",0,2],["w",0,3],["w",1,2],["w",1,3],["c",0,2],["c",1,2],["c",0,3],["c",1,3]],
+    "chunk_at": [-4,-4,-3,-2,-2,-1,0,0,1,1,2,2,5,6,9,10],
+    "cq_at": [-3,-3,-2,-1,-1,-1,0,0,1,1,2,2,5,6,9,10],
+    "chunk_eng": ["v","a","v","v","a","v","v","v","v","v","v","v","v","v","v","v"],
+    "q_at": [3,4,4,5,6,6,7,8],
+    "v_at": [8,9,10,10,11,12,12,13,14,15,15,16,19,19,20,20],
+    "clip_eng": ["a","a","a","a","v","a","v","a","a","v","a","v","v","v","v","v"],
+    "q_eng": ["v","a","v","a","v","a","a","a"],
+    "r_eng": ["a","a","a","a","a","a","a","a","a","a","a","a","a","v","a","v"],
+    "p_eng": ["a","a","a","a","a","a","a","a"],
+    "round_eng": ["v","v","v","v","v","v","v","v","v","v","v","v","v","v","v","v"],
+    "lag": [0,1,0,0,1,0,1,0],
+    "idfc_at": -2,
+    "pe_order": ["pes","co","qturn","fturn","pturn","score"],
+    "ew_order": ["spread","clip","log2","weigh","cq","qout","log1","round","rout","hq","pout","qq","pq"],
+}
+
+
+def tile_localcontextanalysispositivecodegreescor_x1_kernel(tc, tfc, tfw, idfc, idfw, q, out_0, out_1, out_2):
+    nc = tc.nc
+    with ExitStack() as ctx:
+        keep = ctx.enter_context(tc.tile_pool(name="keep", bufs=1))
+        stage = ctx.enter_context(tc.tile_pool(name="stage", bufs=4))
+        psum = ctx.enter_context(tc.psum_pool(name="psum", bufs=2))
+        if MANUAL:
+            ctx.enter_context(tc.manual_schedule())
+
+        w_codes = keep.tile([P, PASSES, SIZE], U32, name="w_codes", align_bytes=64)
+        w_scales = keep.tile([P, PASSES, SIZE], U8, name="w_scales", align_bytes=64)
+        c_codes = keep.tile([P, PASSES, SIZE], U32, name="c_codes", align_bytes=64)
+        c_scales = keep.tile([P, PASSES, SIZE], U8, name="c_scales", align_bytes=64)
+        h_codes = keep.tile([P, PASSES, SIZE], U32, name="h_codes", align_bytes=64)
+        h_scales = keep.tile([P, PASSES, SIZE], U8, name="h_scales", align_bytes=64)
+        q_codes = keep.tile([P, SIZE // P, PASSES * P], U32, name="q_codes", align_bytes=64)
+        q_scales = keep.tile([P, SIZE // P, PASSES * P], U8, name="q_scales", align_bytes=64)
+        p_codes = keep.tile([P, STRIPS, BANK], U32, name="p_codes", align_bytes=64)
+        p_scales = keep.tile([P, STRIPS, BANK], U8, name="p_scales", align_bytes=64)
+
+        w_raw = {}
+        c_raw = {}
+        q_raw = {}
+        live = {}
+
+        def load_w(g, half):
+            t = keep.tile([P, PACK, BANK], BF16, name="w_raw%d%d" % (g, half))
+            rows = tfw[g * K_PASS:(g + 1) * K_PASS, half * BANK:(half + 1) * BANK]
+            nc.sync.dma_start(out=t[:], in_=rows.rearrange("(p j) w -> p j w", j=PACK))
+            w_raw[(g, 2 * half)] = t[:, :, 0:CHUNK]
+            w_raw[(g, 2 * half + 1)] = t[:, :, CHUNK:2 * CHUNK]
+
+        def load_c(g, first, count):
+            t = keep.tile([P, PACK, count * CHUNK], BF16, name="c_raw%d%d" % (g, first))
+            rows = tfc[g * K_PASS:(g + 1) * K_PASS, first * CHUNK:(first + count) * CHUNK]
+            nc.sync.dma_start(out=t[:], in_=rows.rearrange("(p j) c -> p j c", j=PACK))
+            for s in range(count):
+                c_raw[(g, first + s)] = t[:, :, s * CHUNK:(s + 1) * CHUNK]
+
+        def load_q(i):
+            t = keep.tile([P, 2, SIZE], BF16, name="q_raw%d" % i)
+            nc.sync.dma_start(out=t[:], in_=q.rearrange("(j i p) w -> i p j w", j=2, p=P)[i])
+            q_raw[i] = t[:, 0, :]
+            q_raw[i + 4] = t[:, 1, :]
+
+        def spread(which, g, s, eng):
+            raw = (w_raw if which == "w" else c_raw)[(g, s)]
+            t = stage.tile([P, CHUNK, PACK], BF16, name="spread_g" if eng == "g" else "spread", bufs=POOL_BUFS if eng == "g" else 4, align_bytes=64)
+            dst = t[:].rearrange("p (c i) t -> p c t i", i=4)
+            src = raw.rearrange("p t (c i) -> p c t i", i=4)
+            if eng == "v":
+                nc.vector.tensor_copy(out=dst, in_=src)
+            elif eng == "a":
+                nc.scalar.copy(out=dst, in_=src)
+            elif eng in ("V", "A"):
+                evac(eng.replace("V", "v"), t[:].rearrange("p c t -> p (c t)"), live[("sbank", which, g, s)][:])
+            else:
+                nc.gpsimd.tensor_scalar(out=t[:], in0=raw.rearrange("p t c -> p c t"), scalar1=1.0, scalar2=0.0, op0=ALU.mult, op1=ALU.add)
+            live[(which, g, s)] = t
+
+        def pe_spread(which, g, s):
+            raw = (w_raw if which == "w" else c_raw)[(g, s)]
+            bank = psum.tile([P, CHUNK * PACK], BF16, name="r_bank")
+            for b in range(2):
+                nc.tensor.matmul(bank[:, b * BANK:(b + 1) * BANK], lhsT=ident_bf[:],
+                                 rhs=raw[:, :, b * P:(b + 1) * P].rearrange("p t c -> p c t"), start=True, stop=True)
+            live[("sbank", which, g, s)] = bank
+
+        def quant_in(which, g, s):
+            codes, scales = (w_codes, w_scales) if which == "w" else (c_codes, c_scales)
+            cols = slice(s * CHUNK, (s + 1) * CHUNK)
+            nc.vector.quantize_mx(out=codes[:, g, cols].bitcast(FP8X4), scales=scales[:, g, cols],
+                                  in_=live[(which, g, s)][:].rearrange("p c t -> p (c t)"))
+
+        def evac(eng, out, in_):
+            if eng == "v":
+                nc.vector.tensor_copy(out=out, in_=in_)
+            else:
+                nc.scalar.copy(out=out, in_=in_)
+
+        def q_turn(i):
+            bank = psum.tile([P, 4, P], F32, name="turn_bank")
+            words = q_raw[i].bitcast(F32)
+            for g in range(PASSES):
+                for u in range(2):
+                    nc.tensor.transpose(bank[:, 2 * g + u, :], words[:, 256 * g + u:256 * (g + 1):2], ident[:])
+            live[("qbank", i)] = bank
+
+        def q_out(i, eng):
+            t = stage.tile([P, PASSES, P, 2], F32, name="q_words", align_bytes=64)
+            evac(eng, t[:], live[("qbank", i)][:].rearrange("p (g u) r -> p g r u", u=2))
+            live[("qw", i)] = t
+
+        def q_quant(i):
+            nc.vector.quantize_mx(out=q_codes[:, i, :].bitcast(FP8X4), scales=q_scales[:, i, :],
+                                  in_=live[("qw", i)][:].rearrange("p g r u -> p (g r u)").bitcast(BF16))
+
+        def co(n):
+            ci, half = UNITS[n]
+            bank = psum.tile([P, BANK], F32, name="co_bank")
+            m = slice(ci * P, (ci + 1) * P)
+            w = slice(half * BANK, (half + 1) * BANK)
+            for g in range(PASSES):
+                nc.tensor.matmul_mx(out=bank[:], lhsT=c_codes[:, g, m].bitcast(FP8X4), lhsT_scale=c_scales[:, g, m],
+                                    rhs=w_codes[:, g, w].bitcast(FP8X4), rhs_scale=w_scales[:, g, w],
+                                    start=(g == 0), stop=(g == PASSES - 1))
+            live[("co", n)] = bank
+
+        def clip(n, eng):
+            t = stage.tile([P, PACK, P], F32, name="clip")
+            src = live[("co", n)][:].rearrange("c (m t) -> c t m", t=PACK)
+            if eng == "v":
+                nc.vector.tensor_scalar(out=t[:], in0=src, scalar1=1.0 / 32.0, scalar2=0.0, op0=ALU.mult, op1=ALU.max)
+            else:
+                nc.scalar.activation(out=t[:], in_=src, func=ACT.Relu, scale=1.0 / 32.0)
+            live[("clip", n)] = t
+
+        def log1(n):
+            t = stage.tile([P, PACK, P], F32, name="log1")
+            nc.scalar.activation(out=t[:], in_=live[("clip", n)][:], func=ACT.Ln, bias=1.0)
+            live[("log1", n)] = t
+
+        def log2(n):
+            ci = UNITS[n][0]
+            t = stage.tile([P, PACK, P], F32, name="log2")
+            nc.scalar.activation(out=t[:], in_=live[("log1", n)][:], func=ACT.Ln, bias=0.1, scale=idfc_col[:, ci:ci + 1])
+            live[("log2", n)] = t
+
+        def f_turn(n):
+            bank = psum.tile([P, PACK, P], F32, name="f_bank")
+            for t in range(PACK):
+                nc.tensor.transpose(bank[:, t, :], live[("log2", n)][:, t, :], ident[:])
+            live[("fbank", n)] = bank
+
+        def weigh(n):
+            half = UNITS[n][1]
+            t = stage.tile([P, P, PACK], BF16, name="h_bf", align_bytes=64)
+            nc.vector.tensor_tensor(out=t[:], in0=live[("fbank", n)][:].rearrange("p t c -> p c t"),
+                                    in1=idfw_col[:, half:half + 1, :].to_broadcast([P, P, PACK]), op=ALU.mult)
+            live[("h", n)] = t
+
+        def h_quant(n):
+            ci, half = UNITS[n]
+            cols = slice(ci * P, (ci + 1) * P)
+            nc.vector.quantize_mx(out=h_codes[:, half, cols].bitcast(FP8X4), scales=h_scales[:, half, cols],
+                                  in_=live[("h", n)][:].rearrange("p c t -> p (c t)"))
+
+        def score(v):
+            k, i = divmod(v, 4)
+            bank = psum.tile([P, 2, CHUNK], F32, name="r_bank")
+            cols = slice(k * CHUNK, (k + 1) * CHUNK)
+            for j in range(2):
+                for g in range(PASSES):
+                    m = slice(g * P, (g + 1) * P)
+                    nc.tensor.matmul_mx(out=bank[:, j, :], lhsT=q_codes[:, i + 4 * j, m].bitcast(FP8X4), lhsT_scale=q_scales[:, i + 4 * j, m],
+                                        rhs=h_codes[:, g, cols].bitcast(FP8X4), rhs_scale=h_scales[:, g, cols],
+                                        start=(g == 0), stop=(g == PASSES - 1))
+            live[("rbank", v)] = bank
+
+        def r_out(v, eng):
+            k, i = divmod(v, 4)
+            t = stage.tile([P, 2, CHUNK], F32, name="r_f32", bufs=R_BUFS)
+            evac(eng, t[:], live[("rbank", v)][:])
+            live[("r", v)] = t
+            nc.sync.dma_start(out=out_0[:, k * CHUNK:(k + 1) * CHUNK].rearrange("(j i p) c -> i p j c", j=2, p=P)[i], in_=t[:])
+
+        def r_round(v, eng):
+            t = stage.tile([P, 2, P, 2], BF16, name="r_bf")
+            src = live[("r", v)][:].rearrange("q j (p u e) -> q u (j p) e", u=2, e=2)
+            if eng == "v":
+                nc.vector.tensor_copy(out=t[:], in_=src)
+            elif eng == "a":
+                nc.scalar.copy(out=t[:], in_=src)
+            else:
+                nc.gpsimd.tensor_scalar(out=t[:], in0=src, scalar1=1.0, scalar2=0.0, op0=ALU.mult, op1=ALU.add)
+            live[("rb", v)] = t
+
+        def p_turn(v):
+            if v % 2 == 0:
+                live[("pbank", v // 2)] = psum.tile([P, 4, P], F32, name="turn_bank")
+            bank = live[("pbank", v // 2)]
+            words = live[("rb", v)][:].rearrange("q u m e -> q (u m e)").bitcast(F32)
+            for u in range(2):
+                nc.tensor.transpose(bank[:, 2 * (v % 2) + u, :], words[:, u * P:(u + 1) * P], ident[:])
+
+        def p_out(vv, eng):
+            t = stage.tile([P, 2, P, 2], F32, name="p_words", align_bytes=64)
+            evac(eng, t[:], live[("pbank", vv)][:].rearrange("p (i u) r -> p i r u", u=2))
+            live[("pw", vv)] = t
+
+        def p_quant(vv):
+            k, ii = divmod(vv, 2)
+            cols = slice(ii * 2 * P, (ii + 1) * 2 * P)
+            nc.vector.quantize_mx(out=p_codes[:, k, cols].bitcast(FP8X4), scales=p_scales[:, k, cols],
+                                  in_=live[("pw", vv)][:].rearrange("p i r u -> p (i r u)").bitcast(BF16))
+
+        def p_store(k, queues):
+            g, half = divmod(k, 2)
+            words = out_1.rearrange("g p m t -> g p (m t)").bitcast(I32)
+            for j in range(2):
+                queues[j].dma_start(out=words[g, 64 * half:64 * (half + 1), j * BANK:(j + 1) * BANK],
+                                    in_=p_codes[64 * j:64 * (j + 1), k, :].bitcast(I32))
+
+        def s_store(first, count, queues):
+            rows = out_2.rearrange("g (h b r) m -> b r (g h) m", h=2, b=2).bitcast(I32)
+            for quad in range(4):
+                j, b = divmod(quad, 2)
+                queues[quad].dma_start(out=rows[b, :, first:first + count, j * P:(j + 1) * P],
+                                       in_=p_scales[32 * quad:32 * quad + 4, first:first + count, :].bitcast(I32))
+
+        warm = keep.tile([P, 8], F32, name="warm")
+        nc.vector.memset(warm[:], 1.0)
+        warm_out = keep.tile([P, 8], F32, name="warm_out")
+        idfc_rows = keep.tile([P, P], BF16, name="idfc_rows")
+        nc.vector.memset(idfc_rows[:], 0.0)
+        idfw_col = keep.tile([P, PASSES, PACK], BF16, name="idfw_col")
+        nc.scalar.dma_start(out=idfc_rows[0:8, :], in_=idfc.rearrange("(r p) -> r p", p=P))
+        nc.scalar.dma_start(out=idfw_col[:], in_=idfw.rearrange("(g p t) -> p g t", p=P, t=PACK))
+        nc.scalar.activation(out=warm_out[:], in_=warm[:], func=ACT.Ln)
+        ident_bf = keep.tile([P, P], BF16, name="ident_bf")
+        make_identity(nc, ident_bf[:])
+        ident = keep.tile([P, P], F32, name="ident")
+        make_identity(nc, ident[:])
+        idfc_col = keep.tile([P, 8], F32, name="idfc_col")
+
+        def idfc_out():
+            idfc_bank = psum.tile([P, P], BF16, name="turn_bank")
+            nc.tensor.transpose(idfc_bank[:], idfc_rows[:], ident_bf[:])
+            nc.scalar.copy(out=idfc_col[:], in_=idfc_bank[:, 0:8])
+
+        for which, g, first, count in PAR["loads"]:
+            if which == "w":
+                load_w(g, first)
+            elif which == "c":
+                load_c(g, first, count)
+            else:
+                load_q(first)
+
+        chunks = PAR["chunks"]
+        q_order = [0, 4, 1, 5, 2, 6, 3, 7]
+
+        def at(name, s):
+            return [x for x, step in enumerate(PAR[name]) if step == s]
+
+        def unit(s):
+            return [s] if 0 <= s < 16 else []
+
+        lag = PAR["lag"]
+        l_log1 = lag[0]
+        l_log2 = l_log1 + lag[1]
+        l_turn = l_log2 + 1
+        l_weigh = l_turn + lag[2]
+        l_hq = l_weigh + lag[3]
+        l_round = lag[4]
+        l_pturn = l_round + 1
+        l_pout = l_pturn + lag[5]
+        l_pq = l_pout + lag[6]
+
+        def item(name, s):
+            if name == "co":
+                for n in unit(s):
+                    co(n)
+            elif name == "qturn":
+                for x in at("q_at", s):
+                    q_turn(q_order[x])
+            elif name == "fturn":
+                for n in unit(s - l_turn):
+                    f_turn(n)
+            elif name == "pturn":
+                for v in at("v_at", s - l_pturn):
+                    p_turn(v)
+            elif name == "score":
+                for v in at("v_at", s):
+                    score(v)
+            elif name == "pes":
+                for x in at("chunk_at", s):
+                    if PAR["chunk_eng"][x] in ("V", "A"):
+                        pe_spread(*chunks[x])
+            elif name == "spread":
+                for x in at("chunk_at", s):
+                    spread(*chunks[x], PAR["chunk_eng"][x])
+            elif name == "cq":
+                for x in at("cq_at", s):
+                    quant_in(*chunks[x])
+            elif name == "clip":
+                for n in unit(s):
+                    clip(n, PAR["clip_eng"][n])
+            elif name == "log1":
+                for n in unit(s - l_log1):
+                    log1(n)
+            elif name == "log2":
+                for n in unit(s - l_log2):
+                    log2(n)
+            elif name == "weigh":
+                for n in unit(s - l_weigh):
+                    weigh(n)
+            elif name == "hq":
+                for n in unit(s - l_hq):
+                    h_quant(n)
+            elif name == "qout":
+                for x in at("q_at", s):
+                    q_out(q_order[x], PAR["q_eng"][x])
+            elif name == "qq":
+                for x in at("q_at", s - lag[7]):
+                    q_quant(q_order[x])
+            elif name == "rout":
+                for v in at("v_at", s):
+                    r_out(v, PAR["r_eng"][v])
+            elif name == "round":
+                for v in at("v_at", s - l_round):
+                    r_round(v, PAR["round_eng"][v])
+            elif name == "pout":
+                for v in at("v_at", s - l_pout):
+                    if v % 2 == 1:
+                        p_out(v // 2, PAR["p_eng"][v // 2])
+            elif name == "pq":
+                for v in at("v_at", s - l_pq):
+                    if v % 2 == 1:
+                        p_quant(v // 2)
+                    if v == 15:
+                        p_store(3, [nc.sync, nc.scalar])
+                        s_store(3, 1, [nc.sync, nc.scalar, nc.sync, nc.scalar])
+                    elif v % 4 == 3:
+                        p_store(v // 4, [nc.sync, nc.sync])
+                    if v == 11:
+                        s_store(0, 3, [nc.sync] * 4)
+
+        for s in range(-6, 32):
+            if s == PAR["idfc_at"]:
+                idfc_out()
+            for name in PAR["pe_order"] + PAR["ew_order"]:
+                item(name, s)

@@ -24,26 +24,27 @@ FLOPS = 2 * 2 * SIZE * SIZE * SIZE
 
 UNITS = [(0, 0), (1, 0), (2, 0), (3, 0), (0, 1), (1, 1), (2, 1), (3, 1),
          (4, 0), (5, 0), (4, 1), (5, 1), (6, 0), (7, 0), (6, 1), (7, 1)]
-MANUAL = False
+MANUAL = True
 POOL_BUFS = 2
 R_BUFS = 6
 PAR = {
-    "loads": [["w",0,0,1],["c",0,0,1],["w",1,0,1],["c",1,0,1],["c",0,1,1],["c",1,1,1],["w",0,1,1],["w",1,1,1],["q",0,0,1],["q",0,1,1],["q",0,2,1],["q",0,3,1],["c",0,2,2],["c",1,2,2]],
+    "loads": [["w",0,0,1],["c",1,0,1],["c",0,0,1],["w",1,0,1],["c",0,1,1],["c",1,1,1],["w",0,1,1],["w",1,1,1],["q",0,0,1],["c",0,2,2],["c",1,2,2],["q",0,1,1],["q",0,3,1],["q",0,2,1]],
     "chunks": [["w",0,0],["w",0,1],["c",0,0],["w",1,0],["w",1,1],["c",1,0],["c",0,1],["c",1,1],["w",0,2],["w",0,3],["w",1,2],["w",1,3],["c",0,2],["c",1,2],["c",0,3],["c",1,3]],
-    "chunk_at": [-4,-4,-3,-2,-2,-1,0,0,1,1,2,2,5,6,9,10],
-    "cq_at": [-3,-3,-2,-1,-1,-1,0,0,1,1,2,2,5,6,9,10],
-    "chunk_eng": ["v","a","v","v","a","v","v","v","v","v","v","v","v","v","v","v"],
-    "q_at": [3,4,4,5,6,6,7,8],
-    "v_at": [8,9,10,10,11,12,12,13,14,15,15,16,19,19,20,20],
-    "clip_eng": ["a","a","a","a","v","a","v","a","a","v","a","v","v","v","v","v"],
-    "q_eng": ["v","a","v","a","v","a","a","a"],
-    "r_eng": ["a","a","a","a","a","a","a","a","a","a","a","a","a","v","a","v"],
-    "p_eng": ["a","a","a","a","a","a","a","a"],
+    "chunk_at": [-3,-5,-5,-3,-3,-4,-2,-2,0,0,1,1,5,5,6,8],
+    "cq_at": [-3,-4,-5,-3,-2,-4,-1,0,1,2,3,3,6,7,8,10],
+    "chunk_eng": ["A","v","v","A","v","a","A","A","v","v","v","v","v","v","A","A"],
+    "q_at": [4,4,5,7,8,9,10,11],
+    "v_at": [10,10,12,13,13,15,16,16,18,18,19,19,21,21,23,23],
+    "clip_eng": ["a","a","v","a","a","v","v","v","a","a","a","v","v","v","v","v"],
+    "q_eng": ["v","a","a","a","v","a","v","a"],
+    "r_eng": ["v","a","v","a","v","a","a","v","a","a","a","v","a","a","a","a"],
+    "p_eng": ["a","a","a","a","v","a","a","a"],
     "round_eng": ["v","v","v","v","v","v","v","v","v","v","v","v","v","v","v","v"],
-    "lag": [0,1,0,0,1,0,1,0],
-    "idfc_at": -2,
-    "pe_order": ["pes","co","qturn","fturn","pturn","score"],
-    "ew_order": ["spread","clip","log2","weigh","cq","qout","log1","round","rout","hq","pout","qq","pq"],
+    "lag": [2,0,0,1,2,1,0,1],
+    "idfc_at": -3,
+    "pe_order": ["qturn","score","pes","co","pturn","fturn"],
+    "ew_order": ["qq","log1","round","spread","pout","pq","qout","cq","rout","clip","hq","weigh","log2"],
+    "pe_order2": ["pes","score","co","qturn","pturn","fturn"],
 }
 
 
@@ -53,7 +54,9 @@ def tile_localcontextanalysispositivecodegreescor_x1_kernel(tc, tfc, tfw, idfc, 
         keep = ctx.enter_context(tc.tile_pool(name="keep", bufs=1))
         stage = ctx.enter_context(tc.tile_pool(name="stage", bufs=4))
         psum = ctx.enter_context(tc.psum_pool(name="psum", bufs=2))
-        if MANUAL:
+        if MANUAL == "PE":
+            ctx.enter_context(tc.manual_schedule(engines={mybir.EngineType.PE}))
+        elif MANUAL:
             ctx.enter_context(tc.manual_schedule())
 
         w_codes = keep.tile([P, PASSES, SIZE], U32, name="w_codes", align_bytes=64)
@@ -368,14 +371,14 @@ def tile_localcontextanalysispositivecodegreescor_x1_kernel(tc, tfc, tfw, idfc, 
                         p_quant(v // 2)
                     if v == 15:
                         p_store(3, [nc.sync, nc.scalar])
-                        s_store(3, 1, [nc.sync, nc.scalar, nc.sync, nc.scalar])
+                        s_store(2, 2, [nc.sync, nc.scalar, nc.sync, nc.scalar])
                     elif v % 4 == 3:
                         p_store(v // 4, [nc.sync, nc.sync])
-                    if v == 11:
-                        s_store(0, 3, [nc.sync] * 4)
+                    if v == 7:
+                        s_store(0, 2, [nc.sync] * 4)
 
         for s in range(-6, 32):
             if s == PAR["idfc_at"]:
                 idfc_out()
-            for name in PAR["pe_order"] + PAR["ew_order"]:
+            for name in PAR["pe_order2" if s % 2 else "pe_order"] + PAR["ew_order"]:
                 item(name, s)

@@ -26,25 +26,30 @@ UNITS = [(0, 0), (1, 0), (2, 0), (3, 0), (0, 1), (1, 1), (2, 1), (3, 1),
          (4, 0), (5, 0), (4, 1), (5, 1), (6, 0), (7, 0), (6, 1), (7, 1)]
 MANUAL = True
 POOL_BUFS = 2
-R_BUFS = 6
+R_BUFS = 4
 PAR = {
-    "loads": [["w",0,0,1],["c",1,0,1],["c",0,0,1],["w",1,0,1],["c",0,1,1],["c",1,1,1],["w",0,1,1],["w",1,1,1],["q",0,0,1],["c",0,2,2],["c",1,2,2],["q",0,1,1],["q",0,3,1],["q",0,2,1]],
-    "chunks": [["w",0,0],["w",0,1],["c",0,0],["w",1,0],["w",1,1],["c",1,0],["c",0,1],["c",1,1],["w",0,2],["w",0,3],["w",1,2],["w",1,3],["c",0,2],["c",1,2],["c",0,3],["c",1,3]],
-    "chunk_at": [-3,-5,-5,-3,-3,-4,-2,-2,0,0,1,1,5,5,6,8],
-    "cq_at": [-3,-4,-5,-3,-2,-4,-1,0,1,2,3,3,6,7,8,10],
-    "chunk_eng": ["A","v","v","A","v","a","A","A","v","v","v","v","v","v","A","A"],
-    "q_at": [4,4,5,7,8,9,10,11],
-    "v_at": [10,10,12,13,13,15,16,16,18,18,19,19,21,21,23,23],
-    "clip_eng": ["a","a","v","a","a","v","v","v","a","a","a","v","v","v","v","v"],
-    "q_eng": ["v","a","a","a","v","a","v","a"],
-    "r_eng": ["v","a","v","a","v","a","a","v","a","a","a","v","a","a","a","a"],
-    "p_eng": ["a","a","a","a","v","a","a","a"],
+    "loads": [["w",0,0,1],["c",1,0,1],["c",0,0,1],["w",1,0,1],["c",0,1,1],["c",1,1,1],["w",0,1,1],["c",0,2,2],["w",1,1,1],["q",0,0,1],["q",0,3,1],["c",1,2,2],["q",0,1,1],["q",0,2,1]],
+    "chunks": [["w",0,0],["w",0,1],["c",0,0],["w",1,0],["w",1,1],["c",1,0],["c",0,1],["c",1,1],["w",0,2],["w",0,3],["w",1,2],["w",1,3],["c",0,2],["c",0,3],["c",1,2],["c",1,3]],
+    "chunk_at": [-6,-6,-5,-4,-3,-5,-1,-1,-1,-1,0,0,2,3,5,4],
+    "cq_at": [-3,-6,-4,5,-2,-4,-1,-1,3,-1,7,2,2,9,6,11],
+    "chunk_eng": ["v","a","v","v","a","a","a","v","v","v","v","v","v","v","v","v"],
+    "q_at": [3,4,5,6,7,8,9,11],
+    "v_at": [10,11,13,14,14,15,16,16,17,18,19,20,20,20,22,22],
+    "clip_eng": ["a","a","a","a","v","a","a","v","a","a","a","v","a","a","v","a"],
+    "q_eng": ["a","a","a","v","a","v","a","v"],
+    "r_eng": ["v","v","a","v","a","v","a","v","a","a","a","a","v","v","a","a"],
+    "p_eng": ["v","a","a","a","a","a","a","a"],
     "round_eng": ["v","v","v","v","v","v","v","v","v","v","v","v","v","v","v","v"],
-    "lag": [2,0,0,1,2,1,0,1],
+    "lag": [1,0,0,1,1,1,0,2],
     "idfc_at": -3,
-    "pe_order": ["qturn","score","pes","co","pturn","fturn"],
-    "ew_order": ["qq","log1","round","spread","pout","pq","qout","cq","rout","clip","hq","weigh","log2"],
-    "pe_order2": ["pes","score","co","qturn","pturn","fturn"],
+    "pe_order": ["co","score","pes","qturn","pturn","fturn"],
+    "ew_order": ["log1","pout","qq","spread","cq","clip","round","rout","hq","pq","weigh","log2","qout"],
+    "warm_at": [],
+    "b_pair": [0,1,1,1,1,1,1,1],
+    "h_pair": [1,1,1,1,1,1,0,1],
+    "c_pair": [1,1,1,1,1,1,1,0],
+    "p_pair": [1,1,0,0],
+    "s_early": 0,
 }
 
 
@@ -70,6 +75,8 @@ def tile_localcontextanalysispositivecodegreescor_x1_kernel(tc, tfc, tfw, idfc, 
         p_codes = keep.tile([P, STRIPS, BANK], U32, name="p_codes", align_bytes=64)
         p_scales = keep.tile([P, STRIPS, BANK], U8, name="p_scales", align_bytes=64)
 
+        w_grouped = keep.tile([P, PASSES, SIZE, PACK], BF16, name="w_grouped", align_bytes=64)
+        c_grouped = keep.tile([P, PASSES, SIZE, PACK], BF16, name="c_grouped", align_bytes=64)
         w_raw = {}
         c_raw = {}
         q_raw = {}
@@ -79,50 +86,50 @@ def tile_localcontextanalysispositivecodegreescor_x1_kernel(tc, tfc, tfw, idfc, 
             t = keep.tile([P, PACK, BANK], BF16, name="w_raw%d%d" % (g, half))
             rows = tfw[g * K_PASS:(g + 1) * K_PASS, half * BANK:(half + 1) * BANK]
             nc.sync.dma_start(out=t[:], in_=rows.rearrange("(p j) w -> p j w", j=PACK))
-            w_raw[(g, 2 * half)] = t[:, :, 0:CHUNK]
-            w_raw[(g, 2 * half + 1)] = t[:, :, CHUNK:2 * CHUNK]
+            w_raw[(g, 2 * half)] = (t, 0)
+            w_raw[(g, 2 * half + 1)] = (t, 1)
 
         def load_c(g, first, count):
             t = keep.tile([P, PACK, count * CHUNK], BF16, name="c_raw%d%d" % (g, first))
             rows = tfc[g * K_PASS:(g + 1) * K_PASS, first * CHUNK:(first + count) * CHUNK]
             nc.sync.dma_start(out=t[:], in_=rows.rearrange("(p j) c -> p j c", j=PACK))
             for s in range(count):
-                c_raw[(g, first + s)] = t[:, :, s * CHUNK:(s + 1) * CHUNK]
+                c_raw[(g, first + s)] = (t, s)
 
         def load_q(i):
             t = keep.tile([P, 2, SIZE], BF16, name="q_raw%d" % i)
             nc.sync.dma_start(out=t[:], in_=q.rearrange("(j i p) w -> i p j w", j=2, p=P)[i])
-            q_raw[i] = t[:, 0, :]
-            q_raw[i + 4] = t[:, 1, :]
+            q_raw[2 * i] = t[:, 0, :]
+            q_raw[2 * i + 1] = t[:, 1, :]
 
-        def spread(which, g, s, eng):
-            raw = (w_raw if which == "w" else c_raw)[(g, s)]
-            t = stage.tile([P, CHUNK, PACK], BF16, name="spread_g" if eng == "g" else "spread", bufs=POOL_BUFS if eng == "g" else 4, align_bytes=64)
-            dst = t[:].rearrange("p (c i) t -> p c t i", i=4)
+        def spread(which, g, s, count, eng):
+            t, off = (w_raw if which == "w" else c_raw)[(g, s)]
+            raw = t[:, :, off * CHUNK:(off + count) * CHUNK]
+            out = (w_grouped if which == "w" else c_grouped)[:, g, s * CHUNK:(s + count) * CHUNK, :]
+            dst = out.rearrange("p (c i) t -> p c t i", i=4)
             src = raw.rearrange("p t (c i) -> p c t i", i=4)
+            if which == "w":
+                group = w_grouped[:, g, (s // 2) * BANK:(s // 2 + 1) * BANK, :].rearrange("p (i c) t -> p c t i", i=4)
+                dst = group[:, (s % 2) * 64:(s % 2 + count) * 64]
+            for x in range(count):
+                live[(which, g, s + x)] = True
             if eng == "v":
                 nc.vector.tensor_copy(out=dst, in_=src)
             elif eng == "a":
                 nc.scalar.copy(out=dst, in_=src)
-            elif eng in ("V", "A"):
-                evac(eng.replace("V", "v"), t[:].rearrange("p c t -> p (c t)"), live[("sbank", which, g, s)][:])
             else:
-                nc.gpsimd.tensor_scalar(out=t[:], in0=raw.rearrange("p t c -> p c t"), scalar1=1.0, scalar2=0.0, op0=ALU.mult, op1=ALU.add)
-            live[(which, g, s)] = t
+                assert which == "c"
+                nc.gpsimd.tensor_scalar(out=out, in0=raw.rearrange("p t c -> p c t"), scalar1=1.0, scalar2=0.0, op0=ALU.mult, op1=ALU.add)
 
-        def pe_spread(which, g, s):
-            raw = (w_raw if which == "w" else c_raw)[(g, s)]
-            bank = psum.tile([P, CHUNK * PACK], BF16, name="r_bank")
-            for b in range(2):
-                nc.tensor.matmul(bank[:, b * BANK:(b + 1) * BANK], lhsT=ident_bf[:],
-                                 rhs=raw[:, :, b * P:(b + 1) * P].rearrange("p t c -> p c t"), start=True, stop=True)
-            live[("sbank", which, g, s)] = bank
+        def warm_pe():
+            bank = psum.tile([P, BANK], F32, name="r_bank")
+            nc.tensor.matmul(bank[:], lhsT=ident_bf[:], rhs=warm_bf[:], start=True, stop=True)
 
-        def quant_in(which, g, s):
-            codes, scales = (w_codes, w_scales) if which == "w" else (c_codes, c_scales)
-            cols = slice(s * CHUNK, (s + 1) * CHUNK)
+        def quant_in(which, g, s, count):
+            codes, scales, grouped = (w_codes, w_scales, w_grouped) if which == "w" else (c_codes, c_scales, c_grouped)
+            cols = slice(s * CHUNK, (s + count) * CHUNK)
             nc.vector.quantize_mx(out=codes[:, g, cols].bitcast(FP8X4), scales=scales[:, g, cols],
-                                  in_=live[(which, g, s)][:].rearrange("p c t -> p (c t)"))
+                                  in_=grouped[:, g, cols, :].rearrange("p c t -> p (c t)"))
 
         def evac(eng, out, in_):
             if eng == "v":
@@ -138,14 +145,15 @@ def tile_localcontextanalysispositivecodegreescor_x1_kernel(tc, tfc, tfw, idfc, 
                     nc.tensor.transpose(bank[:, 2 * g + u, :], words[:, 256 * g + u:256 * (g + 1):2], ident[:])
             live[("qbank", i)] = bank
 
-        def q_out(i, eng):
-            t = stage.tile([P, PASSES, P, 2], F32, name="q_words", align_bytes=64)
-            evac(eng, t[:], live[("qbank", i)][:].rearrange("p (g u) r -> p g r u", u=2))
-            live[("qw", i)] = t
+        def q_out(x, eng):
+            if x % 2 == 0:
+                live[("qw", x // 2)] = stage.tile([P, 2, PASSES, P, 2], F32, name="q_words", bufs=2, align_bytes=64)
+            evac(eng, live[("qw", x // 2)][:, x % 2], live[("qbank", x)][:].rearrange("p (g u) r -> p g r u", u=2))
 
         def q_quant(i):
-            nc.vector.quantize_mx(out=q_codes[:, i, :].bitcast(FP8X4), scales=q_scales[:, i, :],
-                                  in_=live[("qw", i)][:].rearrange("p g r u -> p (g r u)").bitcast(BF16))
+            nc.vector.quantize_mx(out=q_codes[:, 2 * i:2 * i + 2, :].rearrange("p j m -> p (j m)").bitcast(FP8X4),
+                                  scales=q_scales[:, 2 * i:2 * i + 2, :].rearrange("p j m -> p (j m)"),
+                                  in_=live[("qw", i)][:].rearrange("p j g r u -> p (j g r u)").bitcast(BF16))
 
         def co(n):
             ci, half = UNITS[n]
@@ -159,23 +167,24 @@ def tile_localcontextanalysispositivecodegreescor_x1_kernel(tc, tfc, tfw, idfc, 
             live[("co", n)] = bank
 
         def clip(n, eng):
-            t = stage.tile([P, PACK, P], F32, name="clip")
-            src = live[("co", n)][:].rearrange("c (m t) -> c t m", t=PACK)
+            if n % 2 == 0:
+                live[("clip", n // 2)] = stage.tile([P, 2, PACK, P], F32, name="clip", bufs=3)
+                live[("log1", n // 2)] = stage.tile([P, 2, PACK, P], F32, name="log1", bufs=3)
+            t = live[("clip", n // 2)][:, n % 2]
+            src = live[("co", n)][:].rearrange("c (t m) -> c t m", t=PACK)
             if eng == "v":
-                nc.vector.tensor_scalar(out=t[:], in0=src, scalar1=1.0 / 32.0, scalar2=0.0, op0=ALU.mult, op1=ALU.max)
+                nc.vector.tensor_scalar(out=t, in0=src, scalar1=1.0 / 32.0, scalar2=0.0, op0=ALU.mult, op1=ALU.max)
             else:
-                nc.scalar.activation(out=t[:], in_=src, func=ACT.Relu, scale=1.0 / 32.0)
-            live[("clip", n)] = t
+                nc.scalar.activation(out=t, in_=src, func=ACT.Relu, scale=1.0 / 32.0)
 
-        def log1(n):
-            t = stage.tile([P, PACK, P], F32, name="log1")
-            nc.scalar.activation(out=t[:], in_=live[("clip", n)][:], func=ACT.Ln, bias=1.0)
-            live[("log1", n)] = t
+        def log1(n, count):
+            part = slice(n % 2, n % 2 + count)
+            nc.scalar.activation(out=live[("log1", n // 2)][:, part], in_=live[("clip", n // 2)][:, part], func=ACT.Ln, bias=1.0)
 
         def log2(n):
             ci = UNITS[n][0]
             t = stage.tile([P, PACK, P], F32, name="log2")
-            nc.scalar.activation(out=t[:], in_=live[("log1", n)][:], func=ACT.Ln, bias=0.1, scale=idfc_col[:, ci:ci + 1])
+            nc.scalar.activation(out=t[:], in_=live[("log1", n // 2)][:, n % 2], func=ACT.Ln, bias=0.1, scale=idfc_col[:, ci:ci + 1])
             live[("log2", n)] = t
 
         def f_turn(n):
@@ -186,16 +195,16 @@ def tile_localcontextanalysispositivecodegreescor_x1_kernel(tc, tfc, tfw, idfc, 
 
         def weigh(n):
             half = UNITS[n][1]
-            t = stage.tile([P, P, PACK], BF16, name="h_bf", align_bytes=64)
-            nc.vector.tensor_tensor(out=t[:], in0=live[("fbank", n)][:].rearrange("p t c -> p c t"),
+            if n % 2 == 0:
+                live[("h", n // 2)] = stage.tile([P, 2, P, PACK], BF16, name="h_bf", bufs=3, align_bytes=64)
+            nc.vector.tensor_tensor(out=live[("h", n // 2)][:, n % 2], in0=live[("fbank", n)][:].rearrange("p t c -> p c t"),
                                     in1=idfw_col[:, half:half + 1, :].to_broadcast([P, P, PACK]), op=ALU.mult)
-            live[("h", n)] = t
 
-        def h_quant(n):
+        def h_quant(n, count):
             ci, half = UNITS[n]
-            cols = slice(ci * P, (ci + 1) * P)
+            cols = slice(ci * P, (ci + count) * P)
             nc.vector.quantize_mx(out=h_codes[:, half, cols].bitcast(FP8X4), scales=h_scales[:, half, cols],
-                                  in_=live[("h", n)][:].rearrange("p c t -> p (c t)"))
+                                  in_=live[("h", n // 2)][:, n % 2:n % 2 + count].rearrange("p n c t -> p (n c t)"))
 
         def score(v):
             k, i = divmod(v, 4)
@@ -204,47 +213,50 @@ def tile_localcontextanalysispositivecodegreescor_x1_kernel(tc, tfc, tfw, idfc, 
             for j in range(2):
                 for g in range(PASSES):
                     m = slice(g * P, (g + 1) * P)
-                    nc.tensor.matmul_mx(out=bank[:, j, :], lhsT=q_codes[:, i + 4 * j, m].bitcast(FP8X4), lhsT_scale=q_scales[:, i + 4 * j, m],
+                    nc.tensor.matmul_mx(out=bank[:, j, :], lhsT=q_codes[:, 2 * i + j, m].bitcast(FP8X4), lhsT_scale=q_scales[:, 2 * i + j, m],
                                         rhs=h_codes[:, g, cols].bitcast(FP8X4), rhs_scale=h_scales[:, g, cols],
                                         start=(g == 0), stop=(g == PASSES - 1))
             live[("rbank", v)] = bank
 
         def r_out(v, eng):
             k, i = divmod(v, 4)
-            t = stage.tile([P, 2, CHUNK], F32, name="r_f32", bufs=R_BUFS)
-            evac(eng, t[:], live[("rbank", v)][:])
-            live[("r", v)] = t
-            nc.sync.dma_start(out=out_0[:, k * CHUNK:(k + 1) * CHUNK].rearrange("(j i p) c -> i p j c", j=2, p=P)[i], in_=t[:])
+            if v % 2 == 0:
+                live[("r", v // 2)] = stage.tile([P, 2, 2, CHUNK], F32, name="r_f32", bufs=R_BUFS)
+                live[("rb", v // 2)] = stage.tile([P, 2, 2, P, 2], BF16, name="r_bf", bufs=3)
+            t = live[("r", v // 2)][:, v % 2]
+            evac(eng, t, live[("rbank", v)][:])
+            nc.sync.dma_start(out=out_0[:, k * CHUNK:(k + 1) * CHUNK].rearrange("(j i p) c -> i p j c", j=2, p=P)[i], in_=t)
 
-        def r_round(v, eng):
-            t = stage.tile([P, 2, P, 2], BF16, name="r_bf")
-            src = live[("r", v)][:].rearrange("q j (p u e) -> q u (j p) e", u=2, e=2)
+        def r_round(v, count, eng):
+            part = slice(v % 2, v % 2 + count)
+            dst = live[("rb", v // 2)][:, :, part].rearrange("q u i m e -> q (i m) u e")
+            src = live[("r", v // 2)][:, part].rearrange("q i j (p u e) -> q (i j p) u e", u=2, e=2)
             if eng == "v":
-                nc.vector.tensor_copy(out=t[:], in_=src)
+                nc.vector.tensor_copy(out=dst, in_=src)
             elif eng == "a":
-                nc.scalar.copy(out=t[:], in_=src)
+                nc.scalar.copy(out=dst, in_=src)
             else:
-                nc.gpsimd.tensor_scalar(out=t[:], in0=src, scalar1=1.0, scalar2=0.0, op0=ALU.mult, op1=ALU.add)
-            live[("rb", v)] = t
+                nc.gpsimd.tensor_scalar(out=dst.rearrange("q m u e -> q u m e"), in0=src.rearrange("q m u e -> q u m e"),
+                                        scalar1=1.0, scalar2=0.0, op0=ALU.mult, op1=ALU.add)
 
         def p_turn(v):
             if v % 2 == 0:
                 live[("pbank", v // 2)] = psum.tile([P, 4, P], F32, name="turn_bank")
             bank = live[("pbank", v // 2)]
-            words = live[("rb", v)][:].rearrange("q u m e -> q (u m e)").bitcast(F32)
             for u in range(2):
-                nc.tensor.transpose(bank[:, 2 * (v % 2) + u, :], words[:, u * P:(u + 1) * P], ident[:])
+                words = live[("rb", v // 2)][:, u, v % 2].rearrange("q m e -> q (m e)").bitcast(F32)
+                nc.tensor.transpose(bank[:, 2 * (v % 2) + u, :], words, ident[:])
 
         def p_out(vv, eng):
-            t = stage.tile([P, 2, P, 2], F32, name="p_words", align_bytes=64)
-            evac(eng, t[:], live[("pbank", vv)][:].rearrange("p (i u) r -> p i r u", u=2))
-            live[("pw", vv)] = t
+            if vv % 2 == 0:
+                live[("pw", vv // 2)] = stage.tile([P, 2, 2, P, 2], F32, name="p_words", bufs=2, align_bytes=64)
+            evac(eng, live[("pw", vv // 2)][:, vv % 2], live[("pbank", vv)][:].rearrange("p (i u) r -> p i r u", u=2))
 
-        def p_quant(vv):
+        def p_quant(vv, count):
             k, ii = divmod(vv, 2)
-            cols = slice(ii * 2 * P, (ii + 1) * 2 * P)
+            cols = slice(ii * 2 * P, (ii + count) * 2 * P)
             nc.vector.quantize_mx(out=p_codes[:, k, cols].bitcast(FP8X4), scales=p_scales[:, k, cols],
-                                  in_=live[("pw", vv)][:].rearrange("p i r u -> p (i r u)").bitcast(BF16))
+                                  in_=live[("pw", k)][:, ii:ii + count].rearrange("p a i r u -> p (a i r u)").bitcast(BF16))
 
         def p_store(k, queues):
             g, half = divmod(k, 2)
@@ -271,6 +283,8 @@ def tile_localcontextanalysispositivecodegreescor_x1_kernel(tc, tfc, tfw, idfc, 
         nc.scalar.activation(out=warm_out[:], in_=warm[:], func=ACT.Ln)
         ident_bf = keep.tile([P, P], BF16, name="ident_bf")
         make_identity(nc, ident_bf[:])
+        warm_bf = keep.tile([P, BANK], BF16, name="warm_bf")
+        nc.gpsimd.memset(warm_bf[:], 1.0)
         ident = keep.tile([P, P], F32, name="ident")
         make_identity(nc, ident[:])
         idfc_col = keep.tile([P, 8], F32, name="idfc_col")
@@ -289,13 +303,30 @@ def tile_localcontextanalysispositivecodegreescor_x1_kernel(tc, tfc, tfw, idfc, 
                 load_q(first)
 
         chunks = PAR["chunks"]
-        q_order = [0, 4, 1, 5, 2, 6, 3, 7]
+
+        def runs(xs, engs):
+            out = []
+            for x in xs:
+                which, g, s = chunks[x]
+                if out and out[-1][:2] == [which, g] and out[-1][2] % 2 == 0 and out[-1][2] + 1 == s and out[-1][4] == engs[x] and (which == "w" or s == 3 or engs[x] == "q"):
+                    out[-1][3] = 2
+                else:
+                    out.append([which, g, s, 1, engs[x]])
+            return out
+
+        def paired(name, n):
+            if PAR[name][n // 2]:
+                return [(n - 1, 2)] if n % 2 else []
+            return [(n, 1)]
 
         def at(name, s):
             return [x for x, step in enumerate(PAR[name]) if step == s]
 
         def unit(s):
             return [s] if 0 <= s < 16 else []
+
+        def late(s):
+            return [n for n in range(16) if n + PAR["b_pair"][n // 2] == s]
 
         lag = PAR["lag"]
         l_log1 = lag[0]
@@ -314,53 +345,65 @@ def tile_localcontextanalysispositivecodegreescor_x1_kernel(tc, tfc, tfw, idfc, 
                     co(n)
             elif name == "qturn":
                 for x in at("q_at", s):
-                    q_turn(q_order[x])
+                    q_turn(x)
             elif name == "fturn":
-                for n in unit(s - l_turn):
+                for n in late(s - l_turn):
                     f_turn(n)
             elif name == "pturn":
                 for v in at("v_at", s - l_pturn):
-                    p_turn(v)
+                    for first, count in paired("c_pair", v):
+                        for x in range(first, first + count):
+                            p_turn(x)
             elif name == "score":
                 for v in at("v_at", s):
                     score(v)
             elif name == "pes":
-                for x in at("chunk_at", s):
-                    if PAR["chunk_eng"][x] in ("V", "A"):
-                        pe_spread(*chunks[x])
+                for x in at("warm_at", s):
+                    warm_pe()
             elif name == "spread":
-                for x in at("chunk_at", s):
-                    spread(*chunks[x], PAR["chunk_eng"][x])
+                for job in runs(at("chunk_at", s), PAR["chunk_eng"]):
+                    spread(*job)
             elif name == "cq":
-                for x in at("cq_at", s):
-                    quant_in(*chunks[x])
+                for which, g, first, count, eng in runs(at("cq_at", s), "q" * 16):
+                    if which == "c":
+                        quant_in(which, g, first, count)
+                    elif (first + count) % 2 == 0 and live[(which, g, first + count - 2)] and live[(which, g, first + count - 1)]:
+                        quant_in(which, g, first + count - 2, 2)
             elif name == "clip":
                 for n in unit(s):
                     clip(n, PAR["clip_eng"][n])
             elif name == "log1":
                 for n in unit(s - l_log1):
-                    log1(n)
+                    for job in paired("b_pair", n):
+                        log1(*job)
             elif name == "log2":
                 for n in unit(s - l_log2):
-                    log2(n)
+                    for first, count in paired("b_pair", n):
+                        log2(first)
+                for n in unit(s - l_log2 - 1):
+                    if n % 2 and PAR["b_pair"][n // 2]:
+                        log2(n)
             elif name == "weigh":
-                for n in unit(s - l_weigh):
+                for n in late(s - l_weigh):
                     weigh(n)
             elif name == "hq":
-                for n in unit(s - l_hq):
-                    h_quant(n)
+                for n in late(s - l_hq):
+                    for job in paired("h_pair", n):
+                        h_quant(*job)
             elif name == "qout":
                 for x in at("q_at", s):
-                    q_out(q_order[x], PAR["q_eng"][x])
+                    q_out(x, PAR["q_eng"][x])
             elif name == "qq":
                 for x in at("q_at", s - lag[7]):
-                    q_quant(q_order[x])
+                    if x % 2:
+                        q_quant(x // 2)
             elif name == "rout":
                 for v in at("v_at", s):
                     r_out(v, PAR["r_eng"][v])
             elif name == "round":
                 for v in at("v_at", s - l_round):
-                    r_round(v, PAR["round_eng"][v])
+                    for job in paired("c_pair", v):
+                        r_round(*job, PAR["round_eng"][v])
             elif name == "pout":
                 for v in at("v_at", s - l_pout):
                     if v % 2 == 1:
@@ -368,17 +411,18 @@ def tile_localcontextanalysispositivecodegreescor_x1_kernel(tc, tfc, tfw, idfc, 
             elif name == "pq":
                 for v in at("v_at", s - l_pq):
                     if v % 2 == 1:
-                        p_quant(v // 2)
+                        for job in paired("p_pair", v // 2):
+                            p_quant(*job)
                     if v == 15:
                         p_store(3, [nc.sync, nc.scalar])
-                        s_store(2, 2, [nc.sync, nc.scalar, nc.sync, nc.scalar])
+                        s_store(PAR["s_early"], 4 - PAR["s_early"], [nc.sync, nc.scalar, nc.sync, nc.scalar])
                     elif v % 4 == 3:
                         p_store(v // 4, [nc.sync, nc.sync])
-                    if v == 7:
-                        s_store(0, 2, [nc.sync] * 4)
+                    if v == 4 * PAR["s_early"] - 1:
+                        s_store(0, PAR["s_early"], [nc.sync] * 4)
 
-        for s in range(-6, 32):
+        for s in range(-6, 40):
             if s == PAR["idfc_at"]:
                 idfc_out()
-            for name in PAR["pe_order2" if s % 2 else "pe_order"] + PAR["ew_order"]:
+            for name in PAR["pe_order"] + PAR["ew_order"]:
                 item(name, s)

@@ -18,411 +18,377 @@ PACK = 4
 K_PASS = P * PACK
 PASSES = SIZE // K_PASS
 BANK = 512
-CHUNK = 256
-STRIPS = SIZE // CHUNK
+PSUM_BANKS = 8
+STRIP = 256
+TILES = SIZE // P
 FLOPS = 2 * 2 * SIZE * SIZE * SIZE
 
-UNITS = [(0, 0), (1, 0), (2, 0), (3, 0), (0, 1), (1, 1), (2, 1), (3, 1),
-         (4, 0), (5, 0), (4, 1), (5, 1), (6, 0), (7, 0), (6, 1), (7, 1)]
-MANUAL = True
-POOL_BUFS = 2
-R_BUFS = 4
-PAR = {
-    "loads": [["w",0,0,1],["c",1,0,1],["c",0,0,1],["w",1,0,1],["c",0,1,1],["c",1,1,1],["w",0,1,1],["c",0,2,2],["w",1,1,1],["q",0,0,1],["q",0,3,1],["c",1,2,2],["q",0,1,1],["q",0,2,1]],
-    "chunks": [["w",0,0],["w",0,1],["c",0,0],["w",1,0],["w",1,1],["c",1,0],["c",0,1],["c",1,1],["w",0,2],["w",0,3],["w",1,2],["w",1,3],["c",0,2],["c",0,3],["c",1,2],["c",1,3]],
-    "chunk_at": [-6,-6,-5,-4,-3,-5,-1,-1,-1,-1,0,0,2,3,5,4],
-    "cq_at": [-3,-6,-4,5,-2,-4,-1,-1,3,-1,7,2,2,9,6,11],
-    "chunk_eng": ["v","a","v","v","a","a","a","v","v","v","v","v","v","v","v","v"],
-    "q_at": [3,4,5,6,7,8,9,11],
-    "v_at": [10,11,13,14,14,15,16,16,17,18,19,20,20,20,22,22],
-    "clip_eng": ["a","a","a","a","v","a","a","v","a","a","a","v","a","a","v","a"],
-    "q_eng": ["a","a","a","v","a","v","a","v"],
-    "r_eng": ["v","v","a","v","a","v","a","v","a","a","a","a","v","v","a","a"],
-    "p_eng": ["v","a","a","a","a","a","a","a"],
-    "round_eng": ["v","v","v","v","v","v","v","v","v","v","v","v","v","v","v","v"],
-    "lag": [1,0,0,1,1,1,0,2],
-    "idfc_at": -3,
-    "pe_order": ["co","score","pes","qturn","pturn","fturn"],
-    "ew_order": ["log1","pout","qq","spread","cq","clip","round","rout","hq","pq","weigh","log2","qout"],
-    "warm_at": [],
-    "b_pair": [0,1,1,1,1,1,1,1],
-    "h_pair": [1,1,1,1,1,1,0,1],
-    "c_pair": [1,1,1,1,1,1,1,0],
-    "p_pair": [1,1,0,0],
-    "s_early": 0,
-}
+VECTOR = "vector"
+SCALAR = "scalar"
+
+UNITS = [(tile, half) for half in range(2) for tile in range(4)]
+UNITS = UNITS + [(tile + one, half) for tile in (4, 6) for half in range(2) for one in range(2)]
+SCORES = 16
+
+Q_STEP = 4
+SCORE_STEP = 13
+STEPS = 27
+
+LATE_INTERLEAVES = {2: [(1, 3, VECTOR)], 3: [(0, 2, SCALAR), (1, 2, VECTOR)], 5: [(0, 3, VECTOR)]}
+LATE_QUANTISES = {5: 2, 10: 3}
+
+CLIPS_ON_VECTOR = (4, 8, 12, 15)
+Q_TILES_ON_SCALAR = (4,)
+SCORES_ON_VECTOR = (0, 1, 4, 7, 10)
+OUTPUT_BANKS_ON_VECTOR = (3, 5)
 
 
 def tile_localcontextanalysispositivecodegreescor_x1_kernel(tc, tfc, tfw, idfc, idfw, q, out_0, out_1, out_2):
     nc = tc.nc
     with ExitStack() as ctx:
         keep = ctx.enter_context(tc.tile_pool(name="keep", bufs=1))
-        stage = ctx.enter_context(tc.tile_pool(name="stage", bufs=4))
-        psum = ctx.enter_context(tc.psum_pool(name="psum", bufs=2))
-        if MANUAL == "PE":
-            ctx.enter_context(tc.manual_schedule(engines={mybir.EngineType.PE}))
-        elif MANUAL:
-            ctx.enter_context(tc.manual_schedule())
+        stage = ctx.enter_context(tc.tile_pool(name="stage", bufs=3))
+        psum = ctx.enter_context(tc.psum_pool(name="psum", bufs=PSUM_BANKS))
+        ctx.enter_context(tc.manual_schedule())
 
-        w_codes = keep.tile([P, PASSES, SIZE], U32, name="w_codes", align_bytes=64)
-        w_scales = keep.tile([P, PASSES, SIZE], U8, name="w_scales", align_bytes=64)
-        c_codes = keep.tile([P, PASSES, SIZE], U32, name="c_codes", align_bytes=64)
-        c_scales = keep.tile([P, PASSES, SIZE], U8, name="c_scales", align_bytes=64)
-        h_codes = keep.tile([P, PASSES, SIZE], U32, name="h_codes", align_bytes=64)
-        h_scales = keep.tile([P, PASSES, SIZE], U8, name="h_scales", align_bytes=64)
-        q_codes = keep.tile([P, SIZE // P, PASSES * P], U32, name="q_codes", align_bytes=64)
-        q_scales = keep.tile([P, SIZE // P, PASSES * P], U8, name="q_scales", align_bytes=64)
-        p_codes = keep.tile([P, STRIPS, BANK], U32, name="p_codes", align_bytes=64)
-        p_scales = keep.tile([P, STRIPS, BANK], U8, name="p_scales", align_bytes=64)
+        def planes(name, shape):
+            words = keep.tile(shape, U32, name=name + "_words", align_bytes=64)
+            scales = keep.tile(shape, U8, name=name + "_scales", align_bytes=64)
+            return words, scales
 
-        w_grouped = keep.tile([P, PASSES, SIZE, PACK], BF16, name="w_grouped", align_bytes=64)
-        c_grouped = keep.tile([P, PASSES, SIZE, PACK], BF16, name="c_grouped", align_bytes=64)
-        w_raw = {}
-        c_raw = {}
-        q_raw = {}
-        live = {}
+        def new_bank(shape, dtype):
+            return psum.tile(shape, dtype, name="bank")
 
-        def load_w(g, half):
-            t = keep.tile([P, PACK, BANK], BF16, name="w_raw%d%d" % (g, half))
-            rows = tfw[g * K_PASS:(g + 1) * K_PASS, half * BANK:(half + 1) * BANK]
-            nc.sync.dma_start(out=t[:], in_=rows.rearrange("(p j) w -> p j w", j=PACK))
-            w_raw[(g, 2 * half)] = (t, 0)
-            w_raw[(g, 2 * half + 1)] = (t, 1)
-
-        def load_c(g, first, count):
-            t = keep.tile([P, PACK, count * CHUNK], BF16, name="c_raw%d%d" % (g, first))
-            rows = tfc[g * K_PASS:(g + 1) * K_PASS, first * CHUNK:(first + count) * CHUNK]
-            nc.sync.dma_start(out=t[:], in_=rows.rearrange("(p j) c -> p j c", j=PACK))
-            for s in range(count):
-                c_raw[(g, first + s)] = (t, s)
-
-        def load_q(i):
-            t = keep.tile([P, 2, SIZE], BF16, name="q_raw%d" % i)
-            nc.sync.dma_start(out=t[:], in_=q.rearrange("(j i p) w -> i p j w", j=2, p=P)[i])
-            q_raw[2 * i] = t[:, 0, :]
-            q_raw[2 * i + 1] = t[:, 1, :]
-
-        def spread(which, g, s, count, eng):
-            t, off = (w_raw if which == "w" else c_raw)[(g, s)]
-            raw = t[:, :, off * CHUNK:(off + count) * CHUNK]
-            out = (w_grouped if which == "w" else c_grouped)[:, g, s * CHUNK:(s + count) * CHUNK, :]
-            dst = out.rearrange("p (c i) t -> p c t i", i=4)
-            src = raw.rearrange("p t (c i) -> p c t i", i=4)
-            if which == "w":
-                group = w_grouped[:, g, (s // 2) * BANK:(s // 2 + 1) * BANK, :].rearrange("p (i c) t -> p c t i", i=4)
-                dst = group[:, (s % 2) * 64:(s % 2 + count) * 64]
-            for x in range(count):
-                live[(which, g, s + x)] = True
-            if eng == "v":
-                nc.vector.tensor_copy(out=dst, in_=src)
-            elif eng == "a":
-                nc.scalar.copy(out=dst, in_=src)
-            else:
-                assert which == "c"
-                nc.gpsimd.tensor_scalar(out=out, in0=raw.rearrange("p t c -> p c t"), scalar1=1.0, scalar2=0.0, op0=ALU.mult, op1=ALU.add)
-
-        def warm_pe():
-            bank = psum.tile([P, BANK], F32, name="r_bank")
-            nc.tensor.matmul(bank[:], lhsT=ident_bf[:], rhs=warm_bf[:], start=True, stop=True)
-
-        def quant_in(which, g, s, count):
-            codes, scales, grouped = (w_codes, w_scales, w_grouped) if which == "w" else (c_codes, c_scales, c_grouped)
-            cols = slice(s * CHUNK, (s + count) * CHUNK)
-            nc.vector.quantize_mx(out=codes[:, g, cols].bitcast(FP8X4), scales=scales[:, g, cols],
-                                  in_=grouped[:, g, cols, :].rearrange("p c t -> p (c t)"))
-
-        def evac(eng, out, in_):
-            if eng == "v":
+        def copy_on(engine, out, in_):
+            if engine == VECTOR:
                 nc.vector.tensor_copy(out=out, in_=in_)
             else:
                 nc.scalar.copy(out=out, in_=in_)
 
-        def q_turn(i):
-            bank = psum.tile([P, 4, P], F32, name="turn_bank")
-            words = q_raw[i].bitcast(F32)
+        def quantise(words, scales, values):
+            nc.vector.quantize_mx(out=words.bitcast(FP8X4), scales=scales, in_=values)
+
+        w_words, w_scales = planes("w", [P, PASSES, SIZE])
+        c_words, c_scales = planes("c", [P, PASSES, SIZE])
+        h_words, h_scales = planes("h", [P, PASSES, SIZE])
+        q_words, q_scales = planes("q", [P, TILES, PASSES * P])
+        o_words, o_scales = planes("o", [P, PASSES, SIZE])
+        w_side = keep.tile([P, PASSES, SIZE, PACK], BF16, name="w_side", align_bytes=64)
+        c_side = keep.tile([P, PASSES, SIZE, PACK], BF16, name="c_side", align_bytes=64)
+        rounded = [keep.tile([P, 2, TILES, P, 2], BF16, name="rounded%d" % g) for g in range(PASSES)]
+
+        w_rows = {}
+        c_rows = {}
+        q_rows = {}
+        live = {}
+
+
+        def load_rows(source, loaded, name, g, strip, count):
+            rows = keep.tile([P, PACK, count * STRIP], BF16, name="%s_rows%d%d" % (name, g, strip))
+            block = source[g * K_PASS:(g + 1) * K_PASS, strip * STRIP:(strip + count) * STRIP]
+            nc.sync.dma_start(out=rows[:], in_=block.rearrange("(p t) c -> p t c", t=PACK))
+            for s in range(count):
+                loaded[(g, strip + s)] = (rows, s)
+
+        def load_q(pair):
+            rows = keep.tile([P, 2, SIZE], BF16, name="q_rows%d" % pair)
+            nc.sync.dma_start(out=rows[:], in_=q.rearrange("(i j p) w -> i p j w", j=2, p=P)[pair])
+            for j in range(2):
+                q_rows[2 * pair + j] = rows[:, j, :]
+
+        def neighbours(loaded, g, strip, count):
+            rows, s = loaded[(g, strip)]
+            return rows[:, :, s * STRIP:(s + count) * STRIP].rearrange("p t (m i) -> p m t i", i=4)
+
+        def interleave_w(g, strip, count, engine):
+            half, part = divmod(strip, 2)
+            side = w_side[:, g, half * BANK:(half + 1) * BANK, :].rearrange("p (i m) t -> p m t i", i=4)
+            quarter = STRIP // 4
+            copy_on(engine, side[:, part * quarter:(part + count) * quarter], neighbours(w_rows, g, strip, count))
+
+        def interleave_c(g, strip, engine):
+            side = c_side[:, g, strip * STRIP:(strip + 1) * STRIP, :].rearrange("p (m i) t -> p m t i", i=4)
+            copy_on(engine, side, neighbours(c_rows, g, strip, 1))
+
+        def quantise_w(g, half):
+            cols = slice(half * BANK, (half + 1) * BANK)
+            quantise(w_words[:, g, cols], w_scales[:, g, cols], w_side[:, g, cols, :].rearrange("p c t -> p (c t)"))
+
+        def quantise_c(g, strip):
+            cols = slice(strip * STRIP, (strip + 1) * STRIP)
+            quantise(c_words[:, g, cols], c_scales[:, g, cols], c_side[:, g, cols, :].rearrange("p c t -> p (c t)"))
+
+
+        def q_turn(x):
+            bank = new_bank([P, PASSES * 2, P], F32)
+            pairs = q_rows[x].bitcast(F32)
+            per_pass = K_PASS // 2
             for g in range(PASSES):
                 for u in range(2):
-                    nc.tensor.transpose(bank[:, 2 * g + u, :], words[:, 256 * g + u:256 * (g + 1):2], ident[:])
-            live[("qbank", i)] = bank
+                    nc.tensor.transpose(bank[:, 2 * g + u, :], pairs[:, per_pass * g + u:per_pass * (g + 1):2], ident[:])
+            live[("q_bank", x)] = bank
 
-        def q_out(x, eng):
+        def q_copy(x):
             if x % 2 == 0:
-                live[("qw", x // 2)] = stage.tile([P, 2, PASSES, P, 2], F32, name="q_words", bufs=2, align_bytes=64)
-            evac(eng, live[("qw", x // 2)][:, x % 2], live[("qbank", x)][:].rearrange("p (g u) r -> p g r u", u=2))
+                live[("q_side", x // 2)] = stage.tile([P, 2, PASSES, P, 2], F32, name="q_side", bufs=2, align_bytes=64)
+            engine = SCALAR if x in Q_TILES_ON_SCALAR else VECTOR
+            copy_on(engine, live[("q_side", x // 2)][:, x % 2], live[("q_bank", x)][:].rearrange("p (g u) r -> p g r u", u=2))
 
-        def q_quant(i):
-            nc.vector.quantize_mx(out=q_codes[:, 2 * i:2 * i + 2, :].rearrange("p j m -> p (j m)").bitcast(FP8X4),
-                                  scales=q_scales[:, 2 * i:2 * i + 2, :].rearrange("p j m -> p (j m)"),
-                                  in_=live[("qw", i)][:].rearrange("p j g r u -> p (j g r u)").bitcast(BF16))
+        def q_quantise(pair):
+            tiles = slice(2 * pair, 2 * pair + 2)
+            quantise(q_words[:, tiles, :].rearrange("p j m -> p (j m)"), q_scales[:, tiles, :].rearrange("p j m -> p (j m)"),
+                     live[("q_side", pair)][:].rearrange("p j g r u -> p (j g r u)").bitcast(BF16))
+
 
         def co(n):
-            ci, half = UNITS[n]
-            bank = psum.tile([P, BANK], F32, name="co_bank")
-            m = slice(ci * P, (ci + 1) * P)
-            w = slice(half * BANK, (half + 1) * BANK)
+            tile, half = UNITS[n]
+            bank = new_bank([P, BANK], F32)
+            concepts = slice(tile * P, (tile + 1) * P)
+            words = slice(half * BANK, (half + 1) * BANK)
             for g in range(PASSES):
-                nc.tensor.matmul_mx(out=bank[:], lhsT=c_codes[:, g, m].bitcast(FP8X4), lhsT_scale=c_scales[:, g, m],
-                                    rhs=w_codes[:, g, w].bitcast(FP8X4), rhs_scale=w_scales[:, g, w],
+                nc.tensor.matmul_mx(out=bank[:], lhsT=c_words[:, g, concepts].bitcast(FP8X4), lhsT_scale=c_scales[:, g, concepts],
+                                    rhs=w_words[:, g, words].bitcast(FP8X4), rhs_scale=w_scales[:, g, words],
                                     start=(g == 0), stop=(g == PASSES - 1))
             live[("co", n)] = bank
 
-        def clip(n, eng):
+        def clip(n):
             if n % 2 == 0:
-                live[("clip", n // 2)] = stage.tile([P, 2, PACK, P], F32, name="clip", bufs=3)
-                live[("log1", n // 2)] = stage.tile([P, 2, PACK, P], F32, name="log1", bufs=3)
-            t = live[("clip", n // 2)][:, n % 2]
-            src = live[("co", n)][:].rearrange("c (t m) -> c t m", t=PACK)
-            if eng == "v":
-                nc.vector.tensor_scalar(out=t, in0=src, scalar1=1.0 / 32.0, scalar2=0.0, op0=ALU.mult, op1=ALU.max)
+                live[("clip", n // 2)] = stage.tile([P, 2, BANK], F32, name="clip")
+                live[("log1", n // 2)] = stage.tile([P, 2, BANK], F32, name="log1")
+            out = live[("clip", n // 2)][:, n % 2]
+            if n in CLIPS_ON_VECTOR:
+                nc.vector.tensor_scalar(out=out, in0=live[("co", n)][:], scalar1=1.0 / 32.0, scalar2=0.0, op0=ALU.mult, op1=ALU.max)
             else:
-                nc.scalar.activation(out=t, in_=src, func=ACT.Relu, scale=1.0 / 32.0)
+                nc.scalar.activation(out=out, in_=live[("co", n)][:], func=ACT.Relu, scale=1.0 / 32.0)
 
-        def log1(n, count):
-            part = slice(n % 2, n % 2 + count)
-            nc.scalar.activation(out=live[("log1", n // 2)][:, part], in_=live[("clip", n // 2)][:, part], func=ACT.Ln, bias=1.0)
+        def log1(first, count):
+            part = slice(first % 2, first % 2 + count)
+            nc.scalar.activation(out=live[("log1", first // 2)][:, part], in_=live[("clip", first // 2)][:, part], func=ACT.Ln, bias=1.0)
 
         def log2(n):
-            ci = UNITS[n][0]
-            t = stage.tile([P, PACK, P], F32, name="log2")
-            nc.scalar.activation(out=t[:], in_=live[("log1", n // 2)][:, n % 2], func=ACT.Ln, bias=0.1, scale=idfc_col[:, ci:ci + 1])
-            live[("log2", n)] = t
+            tile = UNITS[n][0]
+            f = stage.tile([P, PACK, P], F32, name="f", bufs=4)
+            nc.scalar.activation(out=f[:].rearrange("c t m -> c (t m)"), in_=live[("log1", n // 2)][:, n % 2], func=ACT.Ln,
+                                 bias=0.1, scale=idfc_col[:, tile:tile + 1])
+            live[("f", n)] = f
 
         def f_turn(n):
-            bank = psum.tile([P, PACK, P], F32, name="f_bank")
+            bank = new_bank([P, PACK, P], F32)
             for t in range(PACK):
-                nc.tensor.transpose(bank[:, t, :], live[("log2", n)][:, t, :], ident[:])
-            live[("fbank", n)] = bank
+                nc.tensor.transpose(bank[:, t, :], live[("f", n)][:, t, :], ident[:])
+            live[("f_bank", n)] = bank
 
         def weigh(n):
             half = UNITS[n][1]
             if n % 2 == 0:
-                live[("h", n // 2)] = stage.tile([P, 2, P, PACK], BF16, name="h_bf", bufs=3, align_bytes=64)
-            nc.vector.tensor_tensor(out=live[("h", n // 2)][:, n % 2], in0=live[("fbank", n)][:].rearrange("p t c -> p c t"),
+                live[("h", n // 2)] = stage.tile([P, 2, P, PACK], BF16, name="h", align_bytes=64)
+            nc.vector.tensor_tensor(out=live[("h", n // 2)][:, n % 2], in0=live[("f_bank", n)][:].rearrange("p t c -> p c t"),
                                     in1=idfw_col[:, half:half + 1, :].to_broadcast([P, P, PACK]), op=ALU.mult)
 
-        def h_quant(n, count):
-            ci, half = UNITS[n]
-            cols = slice(ci * P, (ci + count) * P)
-            nc.vector.quantize_mx(out=h_codes[:, half, cols].bitcast(FP8X4), scales=h_scales[:, half, cols],
-                                  in_=live[("h", n // 2)][:, n % 2:n % 2 + count].rearrange("p n c t -> p (n c t)"))
+        def h_quantise(pair):
+            tile, half = UNITS[2 * pair]
+            cols = slice(tile * P, (tile + 2) * P)
+            quantise(h_words[:, half, cols], h_scales[:, half, cols], live[("h", pair)][:].rearrange("p n c t -> p (n c t)"))
+
+
+        def extent(v):
+            if v < TILES:
+                return v, 1, 0, BANK
+            strip, pair = divmod(v - TILES, TILES // 2)
+            return 2 * pair, 2, BANK + strip * STRIP, STRIP
 
         def score(v):
-            k, i = divmod(v, 4)
-            bank = psum.tile([P, 2, CHUNK], F32, name="r_bank")
-            cols = slice(k * CHUNK, (k + 1) * CHUNK)
-            for j in range(2):
+            first, count, c0, width = extent(v)
+            bank = new_bank([P, BANK], F32)
+            concepts = slice(c0, c0 + width)
+            for j in range(count):
                 for g in range(PASSES):
-                    m = slice(g * P, (g + 1) * P)
-                    nc.tensor.matmul_mx(out=bank[:, j, :], lhsT=q_codes[:, 2 * i + j, m].bitcast(FP8X4), lhsT_scale=q_scales[:, 2 * i + j, m],
-                                        rhs=h_codes[:, g, cols].bitcast(FP8X4), rhs_scale=h_scales[:, g, cols],
+                    queries = slice(g * P, (g + 1) * P)
+                    nc.tensor.matmul_mx(out=bank[:, j * width:(j + 1) * width],
+                                        lhsT=q_words[:, first + j, queries].bitcast(FP8X4), lhsT_scale=q_scales[:, first + j, queries],
+                                        rhs=h_words[:, g, concepts].bitcast(FP8X4), rhs_scale=h_scales[:, g, concepts],
                                         start=(g == 0), stop=(g == PASSES - 1))
-            live[("rbank", v)] = bank
+            live[("score", v)] = bank
 
-        def r_out(v, eng):
-            k, i = divmod(v, 4)
+        def score_store(v):
+            first, count, c0, width = extent(v)
             if v % 2 == 0:
-                live[("r", v // 2)] = stage.tile([P, 2, 2, CHUNK], F32, name="r_f32", bufs=R_BUFS)
-                live[("rb", v // 2)] = stage.tile([P, 2, 2, P, 2], BF16, name="r_bf", bufs=3)
-            t = live[("r", v // 2)][:, v % 2]
-            evac(eng, t, live[("rbank", v)][:])
-            nc.sync.dma_start(out=out_0[:, k * CHUNK:(k + 1) * CHUNK].rearrange("(j i p) c -> i p j c", j=2, p=P)[i], in_=t)
+                live[("result", v // 2)] = stage.tile([P, 2, BANK], F32, name="result", bufs=4)
+            result = live[("result", v // 2)][:, v % 2]
+            copy_on(VECTOR if v in SCORES_ON_VECTOR else SCALAR, result, live[("score", v)][:])
+            rows = out_0[first * P:(first + count) * P, c0:c0 + width]
+            nc.sync.dma_start(out=rows.rearrange("(j p) c -> p j c", p=P), in_=result.rearrange("p (j c) -> p j c", j=count))
 
-        def r_round(v, count, eng):
-            part = slice(v % 2, v % 2 + count)
-            dst = live[("rb", v // 2)][:, :, part].rearrange("q u i m e -> q (i m) u e")
-            src = live[("r", v // 2)][:, part].rearrange("q i j (p u e) -> q (i j p) u e", u=2, e=2)
-            if eng == "v":
-                nc.vector.tensor_copy(out=dst, in_=src)
-            elif eng == "a":
-                nc.scalar.copy(out=dst, in_=src)
-            else:
-                nc.gpsimd.tensor_scalar(out=dst.rearrange("q m u e -> q u m e"), in0=src.rearrange("q m u e -> q u m e"),
-                                        scalar1=1.0, scalar2=0.0, op0=ALU.mult, op1=ALU.add)
+        def score_round(v, scores):
+            first, count, c0, width = extent(v)
+            group, p0 = c0 // BANK, (c0 % BANK) // PACK
+            out = rounded[group][:, :, first:first + scores * count, p0:p0 + width // PACK, :]
+            results = live[("result", v // 2)][:, v % 2:v % 2 + scores]
+            nc.vector.tensor_copy(out=out.rearrange("q u i p e -> q i p u e"),
+                                  in_=results.rearrange("q n (j p u e) -> q (n j) p u e", j=count, u=2, e=2))
 
-        def p_turn(v):
-            if v % 2 == 0:
-                live[("pbank", v // 2)] = psum.tile([P, 4, P], F32, name="turn_bank")
-            bank = live[("pbank", v // 2)]
-            for u in range(2):
-                words = live[("rb", v // 2)][:, u, v % 2].rearrange("q m e -> q (m e)").bitcast(F32)
-                nc.tensor.transpose(bank[:, 2 * (v % 2) + u, :], words, ident[:])
+        def finished_tiles(v):
+            first, count, c0, width = extent(v)
+            if (c0 + width) % BANK:
+                return []
+            return [(c0 // BANK, first + j) for j in range(count)]
 
-        def p_out(vv, eng):
-            if vv % 2 == 0:
-                live[("pw", vv // 2)] = stage.tile([P, 2, 2, P, 2], F32, name="p_words", bufs=2, align_bytes=64)
-            evac(eng, live[("pw", vv // 2)][:, vv % 2], live[("pbank", vv)][:].rearrange("p (i u) r -> p i r u", u=2))
+        def finished_banks(v):
+            return [4 * group + tile // 2 for group, tile in finished_tiles(v) if tile % 2]
 
-        def p_quant(vv, count):
-            k, ii = divmod(vv, 2)
-            cols = slice(ii * 2 * P, (ii + count) * 2 * P)
-            nc.vector.quantize_mx(out=p_codes[:, k, cols].bitcast(FP8X4), scales=p_scales[:, k, cols],
-                                  in_=live[("pw", k)][:, ii:ii + count].rearrange("p a i r u -> p (a i r u)").bitcast(BF16))
+        def o_turn(v):
+            for group, tile in finished_tiles(v):
+                b = 4 * group + tile // 2
+                if tile % 2 == 0:
+                    live[("o_bank", b)] = new_bank([P, 4, P], F32)
+                for u in range(2):
+                    pairs = rounded[group][:, u, tile].rearrange("q p e -> q (p e)").bitcast(F32)
+                    nc.tensor.transpose(live[("o_bank", b)][:, 2 * (tile % 2) + u, :], pairs, ident[:])
 
-        def p_store(k, queues):
-            g, half = divmod(k, 2)
+        def o_copy(b):
+            if b % 2 == 0:
+                live[("o_side", b // 2)] = stage.tile([P, 2, 2, P, 2], F32, name="o_side", bufs=2, align_bytes=64)
+            engine = VECTOR if b in OUTPUT_BANKS_ON_VECTOR else SCALAR
+            copy_on(engine, live[("o_side", b // 2)][:, b % 2], live[("o_bank", b)][:].rearrange("p (i u) r -> p i r u", u=2))
+
+        def o_quantise(b, banks):
+            group, i = divmod(b, 4)
+            cols = slice(i * 2 * P, (i + banks) * 2 * P)
+            side = live[("o_side", b // 2)][:, b % 2:b % 2 + banks]
+            quantise(o_words[:, group, cols], o_scales[:, group, cols], side.rearrange("p a i r u -> p (a i r u)").bitcast(BF16))
+
+        def store_words(group, first_query, queries):
+            cols = slice(first_query, first_query + queries)
             words = out_1.rearrange("g p m t -> g p (m t)").bitcast(I32)
-            for j in range(2):
-                queues[j].dma_start(out=words[g, 64 * half:64 * (half + 1), j * BANK:(j + 1) * BANK],
-                                    in_=p_codes[64 * j:64 * (j + 1), k, :].bitcast(I32))
+            nc.sync.dma_start(out=words[group, :, cols], in_=o_words[:, group, cols].bitcast(I32))
 
-        def s_store(first, count, queues):
-            rows = out_2.rearrange("g (h b r) m -> b r (g h) m", h=2, b=2).bitcast(I32)
-            for quad in range(4):
-                j, b = divmod(quad, 2)
-                queues[quad].dma_start(out=rows[b, :, first:first + count, j * P:(j + 1) * P],
-                                       in_=p_scales[32 * quad:32 * quad + 4, first:first + count, :].bitcast(I32))
+        def store_scales():
+            rows = out_2.rearrange("g (b r) m -> b r g m", r=4).bitcast(I32)
+            for quadrant, queue in enumerate([nc.scalar, nc.scalar, nc.sync, nc.scalar]):
+                queue.dma_start(out=rows[quadrant], in_=o_scales[32 * quadrant:32 * quadrant + 4].bitcast(I32))
 
-        warm = keep.tile([P, 8], F32, name="warm")
-        nc.vector.memset(warm[:], 1.0)
-        warm_out = keep.tile([P, 8], F32, name="warm_out")
+        def in_pairs(index, singles):
+            if index in singles:
+                return [(index, 1)]
+            return [(index - 1, 2)] if index % 2 else []
+
+        ones = keep.tile([P, 8], F32, name="ones")
+        nc.vector.memset(ones[:], 1.0)
         idfc_rows = keep.tile([P, P], BF16, name="idfc_rows")
         nc.vector.memset(idfc_rows[:], 0.0)
+        nc.scalar.dma_start(out=idfc_rows[0:TILES, :], in_=idfc.rearrange("(r p) -> r p", p=P))
         idfw_col = keep.tile([P, PASSES, PACK], BF16, name="idfw_col")
-        nc.scalar.dma_start(out=idfc_rows[0:8, :], in_=idfc.rearrange("(r p) -> r p", p=P))
         nc.scalar.dma_start(out=idfw_col[:], in_=idfw.rearrange("(g p t) -> p g t", p=P, t=PACK))
-        nc.scalar.activation(out=warm_out[:], in_=warm[:], func=ACT.Ln)
-        ident_bf = keep.tile([P, P], BF16, name="ident_bf")
-        make_identity(nc, ident_bf[:])
-        warm_bf = keep.tile([P, BANK], BF16, name="warm_bf")
-        nc.gpsimd.memset(warm_bf[:], 1.0)
+        warm_up = keep.tile([P, 8], F32, name="warm_up")
+        nc.scalar.activation(out=warm_up[:], in_=ones[:], func=ACT.Ln)
+        ident_bf16 = keep.tile([P, P], BF16, name="ident_bf16")
+        make_identity(nc, ident_bf16[:])
         ident = keep.tile([P, P], F32, name="ident")
         make_identity(nc, ident[:])
-        idfc_col = keep.tile([P, 8], F32, name="idfc_col")
 
-        def idfc_out():
-            idfc_bank = psum.tile([P, P], BF16, name="turn_bank")
-            nc.tensor.transpose(idfc_bank[:], idfc_rows[:], ident_bf[:])
-            nc.scalar.copy(out=idfc_col[:], in_=idfc_bank[:, 0:8])
+        load_rows(tfw, w_rows, "w", 0, 0, 2)
+        load_rows(tfc, c_rows, "c", 0, 0, 1)
+        load_rows(tfc, c_rows, "c", 1, 0, 1)
+        load_rows(tfw, w_rows, "w", 1, 0, 2)
+        for g in range(PASSES):
+            load_rows(tfc, c_rows, "c", g, 1, 1)
+        for g in range(PASSES):
+            load_rows(tfw, w_rows, "w", g, 2, 2)
+        for g in range(PASSES):
+            load_rows(tfc, c_rows, "c", g, 2, 2)
+        for pair in range(TILES // 2):
+            load_q(pair)
 
-        for which, g, first, count in PAR["loads"]:
-            if which == "w":
-                load_w(g, first)
-            elif which == "c":
-                load_c(g, first, count)
-            else:
-                load_q(first)
+        interleave_w(0, 0, 2, VECTOR)
+        interleave_c(0, 0, SCALAR)
+        interleave_c(1, 0, VECTOR)
+        quantise_w(0, 0)
+        quantise_c(0, 0)
+        quantise_c(1, 0)
+        interleave_w(1, 0, 1, SCALAR)
+        interleave_w(1, 1, 1, VECTOR)
+        interleave_c(0, 1, SCALAR)
+        quantise_w(1, 0)
+        interleave_c(1, 1, VECTOR)
+        quantise_c(0, 1)
+        quantise_c(1, 1)
 
-        chunks = PAR["chunks"]
+        idfc_bank = new_bank([P, P], BF16)
+        nc.tensor.transpose(idfc_bank[:], idfc_rows[:], ident_bf16[:])
+        idfc_col = keep.tile([P, TILES], F32, name="idfc_col")
+        nc.scalar.copy(out=idfc_col[:], in_=idfc_bank[:, 0:TILES])
 
-        def runs(xs, engs):
-            out = []
-            for x in xs:
-                which, g, s = chunks[x]
-                if out and out[-1][:2] == [which, g] and out[-1][2] % 2 == 0 and out[-1][2] + 1 == s and out[-1][4] == engs[x] and (which == "w" or s == 3 or engs[x] == "q"):
-                    out[-1][3] = 2
-                else:
-                    out.append([which, g, s, 1, engs[x]])
-            return out
+        interleave_w(0, 2, 2, VECTOR)
+        interleave_w(1, 2, 2, VECTOR)
+        quantise_w(0, 1)
 
-        def paired(name, n):
-            if PAR[name][n // 2]:
-                return [(n - 1, 2)] if n % 2 else []
-            return [(n, 1)]
+        single_units = (0, 1, len(UNITS) - 2, len(UNITS) - 1)
+        last_scores = (SCORES - 2, SCORES - 1)
+        last_banks = (2 * TILES // 2 - 2, 2 * TILES // 2 - 1)
 
-        def at(name, s):
-            return [x for x, step in enumerate(PAR[name]) if step == s]
+        def units_at(step, lag):
+            return [n for n in range(len(UNITS)) if n + lag == step]
 
-        def unit(s):
-            return [s] if 0 <= s < 16 else []
+        def held_units_at(step, lag):
+            return [n for n in range(len(UNITS)) if n + lag + (0 if n in single_units else 1) == step]
 
-        def late(s):
-            return [n for n in range(16) if n + PAR["b_pair"][n // 2] == s]
+        def q_tiles_at(step, lag):
+            return [x for x in range(TILES) if Q_STEP + x + lag == step]
 
-        lag = PAR["lag"]
-        l_log1 = lag[0]
-        l_log2 = l_log1 + lag[1]
-        l_turn = l_log2 + 1
-        l_weigh = l_turn + lag[2]
-        l_hq = l_weigh + lag[3]
-        l_round = lag[4]
-        l_pturn = l_round + 1
-        l_pout = l_pturn + lag[5]
-        l_pq = l_pout + lag[6]
+        def scores_at(step, lag):
+            return [v for v in range(SCORES) if SCORE_STEP + v // 2 + lag == step]
 
-        def item(name, s):
-            if name == "co":
-                for n in unit(s):
-                    co(n)
-            elif name == "qturn":
-                for x in at("q_at", s):
-                    q_turn(x)
-            elif name == "fturn":
-                for n in late(s - l_turn):
-                    f_turn(n)
-            elif name == "pturn":
-                for v in at("v_at", s - l_pturn):
-                    for first, count in paired("c_pair", v):
-                        for x in range(first, first + count):
-                            p_turn(x)
-            elif name == "score":
-                for v in at("v_at", s):
-                    score(v)
-            elif name == "pes":
-                for x in at("warm_at", s):
-                    warm_pe()
-            elif name == "spread":
-                for job in runs(at("chunk_at", s), PAR["chunk_eng"]):
-                    spread(*job)
-            elif name == "cq":
-                for which, g, first, count, eng in runs(at("cq_at", s), "q" * 16):
-                    if which == "c":
-                        quant_in(which, g, first, count)
-                    elif (first + count) % 2 == 0 and live[(which, g, first + count - 2)] and live[(which, g, first + count - 1)]:
-                        quant_in(which, g, first + count - 2, 2)
-            elif name == "clip":
-                for n in unit(s):
-                    clip(n, PAR["clip_eng"][n])
-            elif name == "log1":
-                for n in unit(s - l_log1):
-                    for job in paired("b_pair", n):
-                        log1(*job)
-            elif name == "log2":
-                for n in unit(s - l_log2):
-                    for first, count in paired("b_pair", n):
-                        log2(first)
-                for n in unit(s - l_log2 - 1):
-                    if n % 2 and PAR["b_pair"][n // 2]:
-                        log2(n)
-            elif name == "weigh":
-                for n in late(s - l_weigh):
-                    weigh(n)
-            elif name == "hq":
-                for n in late(s - l_hq):
-                    for job in paired("h_pair", n):
-                        h_quant(*job)
-            elif name == "qout":
-                for x in at("q_at", s):
-                    q_out(x, PAR["q_eng"][x])
-            elif name == "qq":
-                for x in at("q_at", s - lag[7]):
-                    if x % 2:
-                        q_quant(x // 2)
-            elif name == "rout":
-                for v in at("v_at", s):
-                    r_out(v, PAR["r_eng"][v])
-            elif name == "round":
-                for v in at("v_at", s - l_round):
-                    for job in paired("c_pair", v):
-                        r_round(*job, PAR["round_eng"][v])
-            elif name == "pout":
-                for v in at("v_at", s - l_pout):
-                    if v % 2 == 1:
-                        p_out(v // 2, PAR["p_eng"][v // 2])
-            elif name == "pq":
-                for v in at("v_at", s - l_pq):
-                    if v % 2 == 1:
-                        for job in paired("p_pair", v // 2):
-                            p_quant(*job)
-                    if v == 15:
-                        p_store(3, [nc.sync, nc.scalar])
-                        s_store(PAR["s_early"], 4 - PAR["s_early"], [nc.sync, nc.scalar, nc.sync, nc.scalar])
-                    elif v % 4 == 3:
-                        p_store(v // 4, [nc.sync, nc.sync])
-                    if v == 4 * PAR["s_early"] - 1:
-                        s_store(0, PAR["s_early"], [nc.sync] * 4)
+        for step in range(STEPS):
+            for n in units_at(step, 0):
+                co(n)
+            for v in scores_at(step, 0):
+                score(v)
+            for v in scores_at(step, 3):
+                o_turn(v)
+            for x in q_tiles_at(step, 0):
+                q_turn(x)
+            for n in held_units_at(step, 2):
+                f_turn(n)
 
-        for s in range(-6, 40):
-            if s == PAR["idfc_at"]:
-                idfc_out()
-            for name in PAR["pe_order"] + PAR["ew_order"]:
-                item(name, s)
+            for x in q_tiles_at(step, 2):
+                if x % 2:
+                    q_quantise(x // 2)
+            for v in scores_at(step, 2):
+                for first, count in in_pairs(v, last_scores):
+                    score_round(first, count)
+            for n in units_at(step, 1):
+                for first, count in in_pairs(n, single_units):
+                    log1(first, count)
+            for n in units_at(step, 0):
+                clip(n)
+            for v in scores_at(step, 6):
+                for b in finished_banks(v):
+                    for first, count in in_pairs(b, last_banks):
+                        o_quantise(first, count)
+                    if b == 3:
+                        store_words(0, 0, SIZE)
+                    if b in (5, 7):
+                        store_words(1, (b - 5) * 2 * P, BANK)
+            for x in q_tiles_at(step, 0):
+                q_copy(x)
+            for v in scores_at(step, 4):
+                for b in finished_banks(v):
+                    o_copy(b)
+            for n in held_units_at(step, 3):
+                if n % 2:
+                    h_quantise(n // 2)
+            for g, strip, engine in LATE_INTERLEAVES.get(step, []):
+                interleave_c(g, strip, engine)
+            if step == 1:
+                quantise_w(1, 1)
+            if step in LATE_QUANTISES:
+                for g in range(PASSES):
+                    quantise_c(g, LATE_QUANTISES[step])
+            for v in scores_at(step, 0):
+                score_store(v)
+            for n in held_units_at(step, 2):
+                weigh(n)
+            for n in held_units_at(step, 1):
+                log2(n)
+
+        store_scales()

@@ -30,17 +30,14 @@ UNITS = [(tile, half) for half in range(2) for tile in range(4)]
 UNITS = UNITS + [(tile + one, half) for tile in (4, 6) for half in range(2) for one in range(2)]
 SCORES = 16
 
-Q_STEP = 4
-SCORE_STEP = 13
-STEPS = 27
+Q_STEPS = [4, 4, 6, 6, 8, 10, 10, 12]
+SCORE_STEPS = [14, 14, 16, 16, 16, 16, 18, 18, 19, 19, 20, 20, 21, 21, 22, 23]
+STEPS = 29
 
-LATE_INTERLEAVES = {2: [(1, 3, VECTOR)], 3: [(0, 2, SCALAR), (1, 2, VECTOR)], 5: [(0, 3, VECTOR)]}
-LATE_QUANTISES = {5: 2, 10: 3}
-
-CLIPS_ON_VECTOR = (4, 8, 12, 15)
-Q_TILES_ON_SCALAR = (4,)
-SCORES_ON_VECTOR = (0, 1, 4, 7, 10)
-OUTPUT_BANKS_ON_VECTOR = (3, 5)
+CLIPS_ON_VECTOR = (4, 6, 9, 10, 11)
+Q_TILES_ON_SCALAR = (3, 4, 6)
+SCORES_ON_VECTOR = (0, 1, 2, 4, 5, 10)
+OUTPUT_BANKS_ON_VECTOR = (5,)
 
 
 def tile_localcontextanalysispositivecodegreescor_x1_kernel(tc, tfc, tfw, idfc, idfw, q, out_0, out_1, out_2):
@@ -106,16 +103,16 @@ def tile_localcontextanalysispositivecodegreescor_x1_kernel(tc, tfc, tfw, idfc, 
             quarter = STRIP // 4
             copy_on(engine, side[:, part * quarter:(part + count) * quarter], neighbours(w_rows, g, strip, count))
 
-        def interleave_c(g, strip, engine):
-            side = c_side[:, g, strip * STRIP:(strip + 1) * STRIP, :].rearrange("p (m i) t -> p m t i", i=4)
-            copy_on(engine, side, neighbours(c_rows, g, strip, 1))
+        def interleave_c(g, strip, count, engine):
+            side = c_side[:, g, strip * STRIP:(strip + count) * STRIP, :].rearrange("p (m i) t -> p m t i", i=4)
+            copy_on(engine, side, neighbours(c_rows, g, strip, count))
 
         def quantise_w(g, half):
             cols = slice(half * BANK, (half + 1) * BANK)
             quantise(w_words[:, g, cols], w_scales[:, g, cols], w_side[:, g, cols, :].rearrange("p c t -> p (c t)"))
 
-        def quantise_c(g, strip):
-            cols = slice(strip * STRIP, (strip + 1) * STRIP)
+        def quantise_c(g, strip, count):
+            cols = slice(strip * STRIP, (strip + count) * STRIP)
             quantise(c_words[:, g, cols], c_scales[:, g, cols], c_side[:, g, cols, :].rearrange("p c t -> p (c t)"))
 
 
@@ -161,9 +158,8 @@ def tile_localcontextanalysispositivecodegreescor_x1_kernel(tc, tfc, tfw, idfc, 
             else:
                 nc.scalar.activation(out=out, in_=live[("co", n)][:], func=ACT.Relu, scale=1.0 / 32.0)
 
-        def log1(first, count):
-            part = slice(first % 2, first % 2 + count)
-            nc.scalar.activation(out=live[("log1", first // 2)][:, part], in_=live[("clip", first // 2)][:, part], func=ACT.Ln, bias=1.0)
+        def log1(pair):
+            nc.scalar.activation(out=live[("log1", pair)][:], in_=live[("clip", pair)][:], func=ACT.Ln, bias=1.0)
 
         def log2(n):
             tile = UNITS[n][0]
@@ -272,13 +268,13 @@ def tile_localcontextanalysispositivecodegreescor_x1_kernel(tc, tfc, tfw, idfc, 
                 return [(index, 1)]
             return [(index - 1, 2)] if index % 2 else []
 
-        ones = keep.tile([P, 8], F32, name="ones")
-        nc.vector.memset(ones[:], 1.0)
         idfc_rows = keep.tile([P, P], BF16, name="idfc_rows")
         nc.vector.memset(idfc_rows[:], 0.0)
         nc.scalar.dma_start(out=idfc_rows[0:TILES, :], in_=idfc.rearrange("(r p) -> r p", p=P))
         idfw_col = keep.tile([P, PASSES, PACK], BF16, name="idfw_col")
         nc.scalar.dma_start(out=idfw_col[:], in_=idfw.rearrange("(g p t) -> p g t", p=P, t=PACK))
+        ones = keep.tile([P, 8], F32, name="ones")
+        nc.vector.memset(ones[:], 1.0)
         warm_up = keep.tile([P, 8], F32, name="warm_up")
         nc.scalar.activation(out=warm_up[:], in_=ones[:], func=ACT.Ln)
         ident_bf16 = keep.tile([P, P], BF16, name="ident_bf16")
@@ -286,109 +282,109 @@ def tile_localcontextanalysispositivecodegreescor_x1_kernel(tc, tfc, tfw, idfc, 
         ident = keep.tile([P, P], F32, name="ident")
         make_identity(nc, ident[:])
 
-        load_rows(tfw, w_rows, "w", 0, 0, 2)
-        load_rows(tfc, c_rows, "c", 0, 0, 1)
+        load_rows(tfw, w_rows, "w", 0, 0, 4)
         load_rows(tfc, c_rows, "c", 1, 0, 1)
+        load_rows(tfc, c_rows, "c", 0, 0, 1)
         load_rows(tfw, w_rows, "w", 1, 0, 2)
-        for g in range(PASSES):
-            load_rows(tfc, c_rows, "c", g, 1, 1)
-        for g in range(PASSES):
-            load_rows(tfw, w_rows, "w", g, 2, 2)
-        for g in range(PASSES):
-            load_rows(tfc, c_rows, "c", g, 2, 2)
-        for pair in range(TILES // 2):
+        load_rows(tfc, c_rows, "c", 0, 1, 1)
+        load_rows(tfc, c_rows, "c", 1, 1, 1)
+        load_rows(tfw, w_rows, "w", 1, 2, 2)
+        load_rows(tfc, c_rows, "c", 1, 2, 2)
+        load_q(0)
+        load_rows(tfc, c_rows, "c", 0, 2, 2)
+        for pair in range(1, TILES // 2):
             load_q(pair)
 
-        interleave_w(0, 0, 2, VECTOR)
-        interleave_c(0, 0, SCALAR)
-        interleave_c(1, 0, VECTOR)
+        interleave_w(0, 0, 1, SCALAR)
+        interleave_w(0, 1, 1, VECTOR)
+        interleave_w(0, 2, 2, VECTOR)
+        interleave_c(1, 0, 1, VECTOR)
         quantise_w(0, 0)
-        quantise_c(0, 0)
-        quantise_c(1, 0)
-        interleave_w(1, 0, 1, SCALAR)
-        interleave_w(1, 1, 1, VECTOR)
-        interleave_c(0, 1, SCALAR)
+        quantise_c(1, 0, 1)
+        interleave_c(0, 0, 1, SCALAR)
+        interleave_w(1, 1, 1, SCALAR)
+        interleave_c(0, 1, 1, SCALAR)
+        interleave_w(1, 0, 1, VECTOR)
+        quantise_c(0, 0, 1)
         quantise_w(1, 0)
-        interleave_c(1, 1, VECTOR)
-        quantise_c(0, 1)
-        quantise_c(1, 1)
 
         idfc_bank = new_bank([P, P], BF16)
         nc.tensor.transpose(idfc_bank[:], idfc_rows[:], ident_bf16[:])
         idfc_col = keep.tile([P, TILES], F32, name="idfc_col")
         nc.scalar.copy(out=idfc_col[:], in_=idfc_bank[:, 0:TILES])
 
-        interleave_w(0, 2, 2, VECTOR)
-        interleave_w(1, 2, 2, VECTOR)
-        quantise_w(0, 1)
+        late_interleaves = {
+            0: [(interleave_c, (1, 1, 1, SCALAR))],
+            1: [(interleave_w, (1, 2, 2, VECTOR))],
+            2: [(interleave_c, (1, 2, 2, VECTOR))],
+            4: [(interleave_c, (0, 2, 2, VECTOR))],
+        }
+        late_quantises = {
+            0: [(quantise_c, (0, 1, 1))],
+            1: [(quantise_c, (1, 1, 1)), (quantise_w, (1, 1))],
+            2: [(quantise_w, (0, 1))],
+            6: [(quantise_c, (0, 2, 2)), (quantise_c, (1, 2, 2))],
+        }
 
-        single_units = (0, 1, len(UNITS) - 2, len(UNITS) - 1)
-        last_scores = (SCORES - 2, SCORES - 1)
-        last_banks = (2 * TILES // 2 - 2, 2 * TILES // 2 - 1)
+        single_scores = (SCORES - 2, SCORES - 1)
+        single_banks = (4, 5, 6, 7)
 
-        def units_at(step, lag):
-            return [n for n in range(len(UNITS)) if n + lag == step]
+        def started(starts, step, lag):
+            return [i for i, start in enumerate(starts) if start + lag == step]
 
-        def held_units_at(step, lag):
-            return [n for n in range(len(UNITS)) if n + lag + (0 if n in single_units else 1) == step]
-
-        def q_tiles_at(step, lag):
-            return [x for x in range(TILES) if Q_STEP + x + lag == step]
-
-        def scores_at(step, lag):
-            return [v for v in range(SCORES) if SCORE_STEP + v // 2 + lag == step]
-
+        unit_steps = range(len(UNITS))
         for step in range(STEPS):
-            for n in units_at(step, 0):
-                co(n)
-            for v in scores_at(step, 0):
-                score(v)
-            for v in scores_at(step, 3):
-                o_turn(v)
-            for x in q_tiles_at(step, 0):
+            for x in started(Q_STEPS, step, 0):
                 q_turn(x)
-            for n in held_units_at(step, 2):
-                f_turn(n)
+            if step % 2:
+                for n in started(unit_steps, step, 4):
+                    f_turn(n)
+            for v in started(SCORE_STEPS, step, 0):
+                score(v)
+            for n in started(unit_steps, step, 0):
+                co(n)
+            if step % 2 == 0:
+                for n in started(unit_steps, step, 4):
+                    f_turn(n)
+            for v in started(SCORE_STEPS, step, 3):
+                o_turn(v)
 
-            for x in q_tiles_at(step, 2):
-                if x % 2:
-                    q_quantise(x // 2)
-            for v in scores_at(step, 2):
-                for first, count in in_pairs(v, last_scores):
+            for n in started(unit_steps, step, 3):
+                log2(n)
+            for n in started(unit_steps, step, 1):
+                if n % 2:
+                    log1(n // 2)
+            for v in started(SCORE_STEPS, step, 2):
+                for first, count in in_pairs(v, single_scores):
                     score_round(first, count)
-            for n in units_at(step, 1):
-                for first, count in in_pairs(n, single_units):
-                    log1(first, count)
-            for n in units_at(step, 0):
-                clip(n)
-            for v in scores_at(step, 6):
+            for x in started(Q_STEPS, step, 0):
+                q_copy(x)
+            for v in started(SCORE_STEPS, step, 5):
                 for b in finished_banks(v):
-                    for first, count in in_pairs(b, last_banks):
+                    for first, count in in_pairs(b, single_banks):
                         o_quantise(first, count)
                     if b == 3:
                         store_words(0, 0, SIZE)
                     if b in (5, 7):
                         store_words(1, (b - 5) * 2 * P, BANK)
-            for x in q_tiles_at(step, 0):
-                q_copy(x)
-            for v in scores_at(step, 4):
+            for job, arguments in late_interleaves.get(step, []):
+                job(*arguments)
+            for x in started(Q_STEPS, step, 2):
+                if x % 2:
+                    q_quantise(x // 2)
+            for v in started(SCORE_STEPS, step, 4):
                 for b in finished_banks(v):
                     o_copy(b)
-            for n in held_units_at(step, 3):
+            for n in started(unit_steps, step, 5):
                 if n % 2:
                     h_quantise(n // 2)
-            for g, strip, engine in LATE_INTERLEAVES.get(step, []):
-                interleave_c(g, strip, engine)
-            if step == 1:
-                quantise_w(1, 1)
-            if step in LATE_QUANTISES:
-                for g in range(PASSES):
-                    quantise_c(g, LATE_QUANTISES[step])
-            for v in scores_at(step, 0):
+            for v in started(SCORE_STEPS, step, 0):
                 score_store(v)
-            for n in held_units_at(step, 2):
+            for job, arguments in late_quantises.get(step, []):
+                job(*arguments)
+            for n in started(unit_steps, step, 0):
+                clip(n)
+            for n in started(unit_steps, step, 4):
                 weigh(n)
-            for n in held_units_at(step, 1):
-                log2(n)
 
         store_scales()

from contextlib import ExitStack

import concourse.mybir as mybir
from concourse.masks import make_identity

F32 = mybir.dt.float32
BF16 = mybir.dt.bfloat16
U32 = mybir.dt.uint32
I32 = mybir.dt.int32
U8 = mybir.dt.uint8
FP8X4 = mybir.dt.float8_e4m3fn_x4
ACT = mybir.ActivationFunctionType
ALU = mybir.AluOpType

SIZE = 1024
P = 128
PACK = 4
K_PASS = P * PACK
PASSES = SIZE // K_PASS
BANK = 512
PSUM_BANKS = 8
STRIP = 256
TILES = SIZE // P
FLOPS = 2 * 2 * SIZE * SIZE * SIZE

VECTOR = "vector"
SCALAR = "scalar"

UNITS = [(tile, half) for half in range(2) for tile in range(4)]
UNITS = UNITS + [(tile + one, half) for tile in (4, 6) for half in range(2) for one in range(2)]
SCORES = 16

Q_STEPS = [4, 4, 6, 6, 8, 10, 10, 12]
SCORE_STEPS = [14, 14, 16, 16, 16, 16, 18, 18, 19, 19, 20, 20, 21, 21, 22, 23]
STEPS = 29

CLIPS_ON_VECTOR = (4, 6, 9, 10, 11)
Q_TILES_ON_SCALAR = (3, 4, 6)
SCORES_ON_VECTOR = (0, 1, 2, 4, 5, 10)
OUTPUT_BANKS_ON_VECTOR = (5,)


def tile_localcontextanalysispositivecodegreescor_x1_kernel(tc, tfc, tfw, idfc, idfw, q, out_0, out_1, out_2):
    nc = tc.nc
    with ExitStack() as ctx:
        keep = ctx.enter_context(tc.tile_pool(name="keep", bufs=1))
        stage = ctx.enter_context(tc.tile_pool(name="stage", bufs=3))
        psum = ctx.enter_context(tc.psum_pool(name="psum", bufs=PSUM_BANKS))
        ctx.enter_context(tc.manual_schedule())

        def planes(name, shape):
            words = keep.tile(shape, U32, name=name + "_words", align_bytes=64)
            scales = keep.tile(shape, U8, name=name + "_scales", align_bytes=64)
            return words, scales

        def new_bank(shape, dtype):
            return psum.tile(shape, dtype, name="bank")

        def copy_on(engine, out, in_):
            if engine == VECTOR:
                nc.vector.tensor_copy(out=out, in_=in_)
            else:
                nc.scalar.copy(out=out, in_=in_)

        def quantise(words, scales, values):
            nc.vector.quantize_mx(out=words.bitcast(FP8X4), scales=scales, in_=values)

        w_words, w_scales = planes("w", [P, PASSES, SIZE])
        c_words, c_scales = planes("c", [P, PASSES, SIZE])
        h_words, h_scales = planes("h", [P, PASSES, SIZE])
        q_words, q_scales = planes("q", [P, TILES, PASSES * P])
        o_words, o_scales = planes("o", [P, PASSES, SIZE])
        w_side = keep.tile([P, PASSES, SIZE, PACK], BF16, name="w_side", align_bytes=64)
        c_side = keep.tile([P, PASSES, SIZE, PACK], BF16, name="c_side", align_bytes=64)
        rounded = [keep.tile([P, 2, TILES, P, 2], BF16, name="rounded%d" % g) for g in range(PASSES)]

        w_rows = {}
        c_rows = {}
        q_rows = {}
        live = {}


        def load_rows(source, loaded, name, g, strip, count):
            rows = keep.tile([P, PACK, count * STRIP], BF16, name="%s_rows%d%d" % (name, g, strip))
            block = source[g * K_PASS:(g + 1) * K_PASS, strip * STRIP:(strip + count) * STRIP]
            nc.sync.dma_start(out=rows[:], in_=block.rearrange("(p t) c -> p t c", t=PACK))
            for s in range(count):
                loaded[(g, strip + s)] = (rows, s)

        def load_q(pair):
            rows = keep.tile([P, 2, SIZE], BF16, name="q_rows%d" % pair)
            nc.sync.dma_start(out=rows[:], in_=q.rearrange("(i j p) w -> i p j w", j=2, p=P)[pair])
            for j in range(2):
                q_rows[2 * pair + j] = rows[:, j, :]

        def neighbours(loaded, g, strip, count):
            rows, s = loaded[(g, strip)]
            return rows[:, :, s * STRIP:(s + count) * STRIP].rearrange("p t (m i) -> p m t i", i=4)

        def interleave_w(g, strip, count, engine):
            half, part = divmod(strip, 2)
            side = w_side[:, g, half * BANK:(half + 1) * BANK, :].rearrange("p (i m) t -> p m t i", i=4)
            quarter = STRIP // 4
            copy_on(engine, side[:, part * quarter:(part + count) * quarter], neighbours(w_rows, g, strip, count))

        def interleave_c(g, strip, count, engine):
            side = c_side[:, g, strip * STRIP:(strip + count) * STRIP, :].rearrange("p (m i) t -> p m t i", i=4)
            copy_on(engine, side, neighbours(c_rows, g, strip, count))

        def quantise_w(g, half):
            cols = slice(half * BANK, (half + 1) * BANK)
            quantise(w_words[:, g, cols], w_scales[:, g, cols], w_side[:, g, cols, :].rearrange("p c t -> p (c t)"))

        def quantise_c(g, strip, count):
            cols = slice(strip * STRIP, (strip + count) * STRIP)
            quantise(c_words[:, g, cols], c_scales[:, g, cols], c_side[:, g, cols, :].rearrange("p c t -> p (c t)"))


        def q_turn(x):
            bank = new_bank([P, PASSES * 2, P], F32)
            pairs = q_rows[x].bitcast(F32)
            per_pass = K_PASS // 2
            for g in range(PASSES):
                for u in range(2):
                    nc.tensor.transpose(bank[:, 2 * g + u, :], pairs[:, per_pass * g + u:per_pass * (g + 1):2], ident[:])
            live[("q_bank", x)] = bank

        def q_copy(x):
            if x % 2 == 0:
                live[("q_side", x // 2)] = stage.tile([P, 2, PASSES, P, 2], F32, name="q_side", bufs=2, align_bytes=64)
            engine = SCALAR if x in Q_TILES_ON_SCALAR else VECTOR
            copy_on(engine, live[("q_side", x // 2)][:, x % 2], live[("q_bank", x)][:].rearrange("p (g u) r -> p g r u", u=2))

        def q_quantise(pair):
            tiles = slice(2 * pair, 2 * pair + 2)
            quantise(q_words[:, tiles, :].rearrange("p j m -> p (j m)"), q_scales[:, tiles, :].rearrange("p j m -> p (j m)"),
                     live[("q_side", pair)][:].rearrange("p j g r u -> p (j g r u)").bitcast(BF16))


        def co(n):
            tile, half = UNITS[n]
            bank = new_bank([P, BANK], F32)
            concepts = slice(tile * P, (tile + 1) * P)
            words = slice(half * BANK, (half + 1) * BANK)
            for g in range(PASSES):
                nc.tensor.matmul_mx(out=bank[:], lhsT=c_words[:, g, concepts].bitcast(FP8X4), lhsT_scale=c_scales[:, g, concepts],
                                    rhs=w_words[:, g, words].bitcast(FP8X4), rhs_scale=w_scales[:, g, words],
                                    start=(g == 0), stop=(g == PASSES - 1))
            live[("co", n)] = bank

        def clip(n):
            if n % 2 == 0:
                live[("clip", n // 2)] = stage.tile([P, 2, BANK], F32, name="clip")
                live[("log1", n // 2)] = stage.tile([P, 2, BANK], F32, name="log1")
            out = live[("clip", n // 2)][:, n % 2]
            if n in CLIPS_ON_VECTOR:
                nc.vector.tensor_scalar(out=out, in0=live[("co", n)][:], scalar1=1.0 / 32.0, scalar2=0.0, op0=ALU.mult, op1=ALU.max)
            else:
                nc.scalar.activation(out=out, in_=live[("co", n)][:], func=ACT.Relu, scale=1.0 / 32.0)

        def log1(pair):
            nc.scalar.activation(out=live[("log1", pair)][:], in_=live[("clip", pair)][:], func=ACT.Ln, bias=1.0)

        def log2(n):
            tile = UNITS[n][0]
            f = stage.tile([P, PACK, P], F32, name="f", bufs=4)
            nc.scalar.activation(out=f[:].rearrange("c t m -> c (t m)"), in_=live[("log1", n // 2)][:, n % 2], func=ACT.Ln,
                                 bias=0.1, scale=idfc_col[:, tile:tile + 1])
            live[("f", n)] = f

        def f_turn(n):
            bank = new_bank([P, PACK, P], F32)
            for t in range(PACK):
                nc.tensor.transpose(bank[:, t, :], live[("f", n)][:, t, :], ident[:])
            live[("f_bank", n)] = bank

        def weigh(n):
            half = UNITS[n][1]
            if n % 2 == 0:
                live[("h", n // 2)] = stage.tile([P, 2, P, PACK], BF16, name="h", align_bytes=64)
            nc.vector.tensor_tensor(out=live[("h", n // 2)][:, n % 2], in0=live[("f_bank", n)][:].rearrange("p t c -> p c t"),
                                    in1=idfw_col[:, half:half + 1, :].to_broadcast([P, P, PACK]), op=ALU.mult)

        def h_quantise(pair):
            tile, half = UNITS[2 * pair]
            cols = slice(tile * P, (tile + 2) * P)
            quantise(h_words[:, half, cols], h_scales[:, half, cols], live[("h", pair)][:].rearrange("p n c t -> p (n c t)"))


        def extent(v):
            if v < TILES:
                return v, 1, 0, BANK
            strip, pair = divmod(v - TILES, TILES // 2)
            return 2 * pair, 2, BANK + strip * STRIP, STRIP

        def score(v):
            first, count, c0, width = extent(v)
            bank = new_bank([P, BANK], F32)
            concepts = slice(c0, c0 + width)
            for j in range(count):
                for g in range(PASSES):
                    queries = slice(g * P, (g + 1) * P)
                    nc.tensor.matmul_mx(out=bank[:, j * width:(j + 1) * width],
                                        lhsT=q_words[:, first + j, queries].bitcast(FP8X4), lhsT_scale=q_scales[:, first + j, queries],
                                        rhs=h_words[:, g, concepts].bitcast(FP8X4), rhs_scale=h_scales[:, g, concepts],
                                        start=(g == 0), stop=(g == PASSES - 1))
            live[("score", v)] = bank

        def score_store(v):
            first, count, c0, width = extent(v)
            if v % 2 == 0:
                live[("result", v // 2)] = stage.tile([P, 2, BANK], F32, name="result", bufs=4)
            result = live[("result", v // 2)][:, v % 2]
            copy_on(VECTOR if v in SCORES_ON_VECTOR else SCALAR, result, live[("score", v)][:])
            rows = out_0[first * P:(first + count) * P, c0:c0 + width]
            nc.sync.dma_start(out=rows.rearrange("(j p) c -> p j c", p=P), in_=result.rearrange("p (j c) -> p j c", j=count))

        def score_round(v, scores):
            first, count, c0, width = extent(v)
            group, p0 = c0 // BANK, (c0 % BANK) // PACK
            out = rounded[group][:, :, first:first + scores * count, p0:p0 + width // PACK, :]
            results = live[("result", v // 2)][:, v % 2:v % 2 + scores]
            nc.vector.tensor_copy(out=out.rearrange("q u i p e -> q i p u e"),
                                  in_=results.rearrange("q n (j p u e) -> q (n j) p u e", j=count, u=2, e=2))

        def finished_tiles(v):
            first, count, c0, width = extent(v)
            if (c0 + width) % BANK:
                return []
            return [(c0 // BANK, first + j) for j in range(count)]

        def finished_banks(v):
            return [4 * group + tile // 2 for group, tile in finished_tiles(v) if tile % 2]

        def o_turn(v):
            for group, tile in finished_tiles(v):
                b = 4 * group + tile // 2
                if tile % 2 == 0:
                    live[("o_bank", b)] = new_bank([P, 4, P], F32)
                for u in range(2):
                    pairs = rounded[group][:, u, tile].rearrange("q p e -> q (p e)").bitcast(F32)
                    nc.tensor.transpose(live[("o_bank", b)][:, 2 * (tile % 2) + u, :], pairs, ident[:])

        def o_copy(b):
            if b % 2 == 0:
                live[("o_side", b // 2)] = stage.tile([P, 2, 2, P, 2], F32, name="o_side", bufs=2, align_bytes=64)
            engine = VECTOR if b in OUTPUT_BANKS_ON_VECTOR else SCALAR
            copy_on(engine, live[("o_side", b // 2)][:, b % 2], live[("o_bank", b)][:].rearrange("p (i u) r -> p i r u", u=2))

        def o_quantise(b, banks):
            group, i = divmod(b, 4)
            cols = slice(i * 2 * P, (i + banks) * 2 * P)
            side = live[("o_side", b // 2)][:, b % 2:b % 2 + banks]
            quantise(o_words[:, group, cols], o_scales[:, group, cols], side.rearrange("p a i r u -> p (a i r u)").bitcast(BF16))

        def store_words(group, first_query, queries):
            cols = slice(first_query, first_query + queries)
            words = out_1.rearrange("g p m t -> g p (m t)").bitcast(I32)
            nc.sync.dma_start(out=words[group, :, cols], in_=o_words[:, group, cols].bitcast(I32))

        def store_scales():
            rows = out_2.rearrange("g (b r) m -> b r g m", r=4).bitcast(I32)
            for quadrant, queue in enumerate([nc.scalar, nc.scalar, nc.sync, nc.scalar]):
                queue.dma_start(out=rows[quadrant], in_=o_scales[32 * quadrant:32 * quadrant + 4].bitcast(I32))

        def in_pairs(index, singles):
            if index in singles:
                return [(index, 1)]
            return [(index - 1, 2)] if index % 2 else []

        idfc_rows = keep.tile([P, P], BF16, name="idfc_rows")
        nc.vector.memset(idfc_rows[:], 0.0)
        nc.scalar.dma_start(out=idfc_rows[0:TILES, :], in_=idfc.rearrange("(r p) -> r p", p=P))
        idfw_col = keep.tile([P, PASSES, PACK], BF16, name="idfw_col")
        nc.scalar.dma_start(out=idfw_col[:], in_=idfw.rearrange("(g p t) -> p g t", p=P, t=PACK))
        ones = keep.tile([P, 8], F32, name="ones")
        nc.vector.memset(ones[:], 1.0)
        warm_up = keep.tile([P, 8], F32, name="warm_up")
        nc.scalar.activation(out=warm_up[:], in_=ones[:], func=ACT.Ln)
        ident_bf16 = keep.tile([P, P], BF16, name="ident_bf16")
        make_identity(nc, ident_bf16[:])
        ident = keep.tile([P, P], F32, name="ident")
        make_identity(nc, ident[:])

        load_rows(tfw, w_rows, "w", 0, 0, 4)
        load_rows(tfc, c_rows, "c", 1, 0, 1)
        load_rows(tfc, c_rows, "c", 0, 0, 1)
        load_rows(tfw, w_rows, "w", 1, 0, 2)
        load_rows(tfc, c_rows, "c", 0, 1, 1)
        load_rows(tfc, c_rows, "c", 1, 1, 1)
        load_rows(tfw, w_rows, "w", 1, 2, 2)
        load_rows(tfc, c_rows, "c", 1, 2, 2)
        load_q(0)
        load_rows(tfc, c_rows, "c", 0, 2, 2)
        for pair in range(1, TILES // 2):
            load_q(pair)

        interleave_w(0, 0, 1, SCALAR)
        interleave_w(0, 1, 1, VECTOR)
        interleave_w(0, 2, 2, VECTOR)
        interleave_c(1, 0, 1, VECTOR)
        quantise_w(0, 0)
        quantise_c(1, 0, 1)
        interleave_c(0, 0, 1, SCALAR)
        interleave_w(1, 1, 1, SCALAR)
        interleave_c(0, 1, 1, SCALAR)
        interleave_w(1, 0, 1, VECTOR)
        quantise_c(0, 0, 1)
        quantise_w(1, 0)

        idfc_bank = new_bank([P, P], BF16)
        nc.tensor.transpose(idfc_bank[:], idfc_rows[:], ident_bf16[:])
        idfc_col = keep.tile([P, TILES], F32, name="idfc_col")
        nc.scalar.copy(out=idfc_col[:], in_=idfc_bank[:, 0:TILES])

        late_interleaves = {
            0: [(interleave_c, (1, 1, 1, SCALAR))],
            1: [(interleave_w, (1, 2, 2, VECTOR))],
            2: [(interleave_c, (1, 2, 2, VECTOR))],
            4: [(interleave_c, (0, 2, 2, VECTOR))],
        }
        late_quantises = {
            0: [(quantise_c, (0, 1, 1))],
            1: [(quantise_c, (1, 1, 1)), (quantise_w, (1, 1))],
            2: [(quantise_w, (0, 1))],
            6: [(quantise_c, (0, 2, 2)), (quantise_c, (1, 2, 2))],
        }

        single_scores = (SCORES - 2, SCORES - 1)
        single_banks = (4, 5, 6, 7)

        def started(starts, step, lag):
            return [i for i, start in enumerate(starts) if start + lag == step]

        unit_steps = range(len(UNITS))
        for step in range(STEPS):
            for x in started(Q_STEPS, step, 0):
                q_turn(x)
            if step % 2:
                for n in started(unit_steps, step, 4):
                    f_turn(n)
            for v in started(SCORE_STEPS, step, 0):
                score(v)
            for n in started(unit_steps, step, 0):
                co(n)
            if step % 2 == 0:
                for n in started(unit_steps, step, 4):
                    f_turn(n)
            for v in started(SCORE_STEPS, step, 3):
                o_turn(v)

            for n in started(unit_steps, step, 3):
                log2(n)
            for n in started(unit_steps, step, 1):
                if n % 2:
                    log1(n // 2)
            for v in started(SCORE_STEPS, step, 2):
                for first, count in in_pairs(v, single_scores):
                    score_round(first, count)
            for x in started(Q_STEPS, step, 0):
                q_copy(x)
            for v in started(SCORE_STEPS, step, 5):
                for b in finished_banks(v):
                    for first, count in in_pairs(b, single_banks):
                        o_quantise(first, count)
                    if b == 3:
                        store_words(0, 0, SIZE)
                    if b in (5, 7):
                        store_words(1, (b - 5) * 2 * P, BANK)
            for job, arguments in late_interleaves.get(step, []):
                job(*arguments)
            for x in started(Q_STEPS, step, 2):
                if x % 2:
                    q_quantise(x // 2)
            for v in started(SCORE_STEPS, step, 4):
                for b in finished_banks(v):
                    o_copy(b)
            for n in started(unit_steps, step, 5):
                if n % 2:
                    h_quantise(n // 2)
            for v in started(SCORE_STEPS, step, 0):
                score_store(v)
            for job, arguments in late_quantises.get(step, []):
                job(*arguments)
            for n in started(unit_steps, step, 0):
                clip(n)
            for n in started(unit_steps, step, 4):
                weigh(n)

        store_scales()
